import numpy as np, ml_dtypes
CORES = [9,25,41,57]
N = 4
BF = ml_dtypes.bfloat16
C, T, S, DQ = 2048, 256, 4, 3
PL = N * C; FREE = 31
RANGES = (("mem", 0, 63), ("h", 0, 63), ("pnd", 0, PL - 1), ("due", 0, FREE), ("val", 0, 63), ("w", 0, 255), ("kap", 0, 255), ("th", 0, 1008))
def parts(rng):
    tops = rng.integers(24, 64, (1, 8, 16))
    nm = np.add.accumulate(rng.integers(1, PL // 16, (N, 8, T, 16)), axis=3) + rng.integers(0, PL, (N, 8, T, 1))
    nm = rng.permuted(nm & (PL - 1), axis=3)
    du = np.where(rng.random((N, 8, T, 16)) < 0.2, FREE, rng.integers(0, 9, (N, 8, T, 16))); du[..., :S] = FREE
    return {"mem": (rng.random((N, 8, 16, C)) * (tops[..., None] + 1)).astype(np.int64), "h": rng.integers(0, 64, (N, 8, 16, T)),
            "val": (rng.random((N, 8, 16, T, 16)) * (tops[..., None, None] + 1)).astype(np.int64), "nm": nm, "du": du,
            "w": rng.integers(0, 256, (N, 8, 16)), "kap": rng.integers(0, 256, (N, 8, 16)),
            "th": (np.sum(tops, axis=2) * (0.8 + 0.13 * rng.random((N, 8)))).astype(np.int64)}
def pack(p):
    bf = lambda a: np.ascontiguousarray(a).astype(np.float32).astype(BF)
    i4 = lambda a: np.ascontiguousarray(a).astype(np.int32)
    return {"mem": bf(p["mem"].reshape(N, 128, C)), "h": bf(p["h"].reshape(N, 128, T)),
            "pnd": i4(p["nm"].transpose(0, 1, 3, 2).reshape(N, 128, T)), "due": i4(p["du"].transpose(0, 1, 3, 2).reshape(N, 128, T)),
            "val": bf(p["val"].reshape(N, 128, 16 * T)), "w": i4(p["w"].reshape(N, 128, 1)), "kap": i4(p["kap"].reshape(N, 128, 1)),
            "th": i4(np.repeat(p["th"].reshape(N, 8, 1), 16, axis=2).reshape(N, 128, 1))}
def setup_inputs(rng):
    return pack(parts(rng))
def setup_inputs_corners(rng):
    p = parts(rng); s = np.arange(16); own = p["nm"]; mode = rng.integers(0, 7, (N, 8, T, 1)); mode[..., T - 1, 0] = 4; mode[..., 0, 0] = 1
    e = rng.integers(0, S + 1, (N, 8, T, 1)); q = rng.choice(np.array([0, 1, S - 1, S, 30]), (N, 8, T, 16))
    late = 30 - (rng.random((N, 8, T, 16)) * rng.integers(2, 16, (N, 8, T, 1))).astype(np.int64)
    border = C * rng.integers(0, N, (N, 8, T, 1)) - 8; border[..., T - 1, 0] = -8
    du = np.where(mode == 3, np.where(s == 15, 0, FREE), q); du = np.where(mode == 6, late, du)
    du = np.where(mode == 2, np.where(s == 15, e, 30), du); du = np.where(mode == 1, e, du); du = np.where(mode == 0, FREE, du)
    du[..., :S] = FREE
    nm = np.where(mode == 4, (border + s) & (PL - 1), own)
    nm = np.where(mode == 0, (PL - 1) * rng.integers(0, 2, (N, 8, T, 16)), nm)
    p["w"][:, 2] = 0; p["w"][:, 5] = 255; p["kap"][:, 3] = 0; p["kap"][:, 4] = 255; p["th"][:, 1] = 0; p["th"][:, 6] = 1008
    p["th"][1:3] = 1008
    z = slice(T - 8, T); nm[2, 2, z] = own[2, 2, z]; du[2, 2, z] = FREE; du[2, 2, z, 13] = 30; du[2, 2, z, 15] = 0
    p["val"][2, 2, :, z, 13] = 63; p["val"][2, 2, :, z, 15] = 0
    nm[1, 5] = own[1, 5]; du[1, 5, :, S:] = 30
    p["th"][0, 0] = 0; du[0, 0] = FREE
    for r in (0, N - 1):
        p["th"][r, 4] = 0; nm[r, 4] = own[0, 4]; du[r, 4] = FREE; du[r, 4, :, 15] = 0
    du[0, 4, :, 14] = 1
    p["nm"] = nm; p["du"] = du
    return pack(p)
def setup_inputs_crowd(rng):
    p = parts(rng); s = np.arange(16); i = np.arange(T).reshape(1, 1, T, 1); r = np.arange(N).reshape(N, 1, 1, 1)
    owner = rng.integers(0, N, (N, 8, 1, 1)); owner[:, 2] = 0; owner[:, 5] = N - 1; owner[N - 1] = 0
    col = np.broadcast_to(64 + i + 17 * s, (N, 8, T, 16)).copy(); far = (T * (r + 1) + i + 17 * s) % C
    col[:, 2] = far[:, 0]; col[:, 5] = far[:, 0]
    p["nm"] = C * owner + col
    du = np.zeros((N, 8, T, 16), np.int64); du[..., :S] = FREE; du[:, 2, :, 1::2] = FREE; du[N - 1, :, :, 1::2] = FREE; p["du"] = du
    p["w"][:, 2] = 0; p["w"][N - 1] = 0; p["th"][:] = 0
    return pack(p)
def edge(rng, a, b):
    k = rng.integers(0, 3, a)
    return 63 * np.where(k == 2, rng.integers(0, 2, b), k)
def setup_inputs_ends(rng):
    p = parts(rng); s = np.arange(16)
    mem = edge(rng, (N, 8, 1, C), (N, 8, 16, C)); mem[..., 0] = 0; mem[..., C - 1] = 63
    h = edge(rng, (N, 8, 1, T), (N, 8, 16, T)); val = edge(rng, (N, 8, 1, T, 16), (N, 8, 16, T, 16))
    for g in (1, 5, 7): mem[:, g, 3] = 0
    for g in (1, 5): val[:, g, 3] = 0
    w = 255 * rng.integers(0, 2, (N, 8, 16)); w[:, 1::2, 15] = 65; w[:, 6] = 255
    kap = 255 * rng.integers(0, 2, (N, 8, 16)); kap[:, 1::2, 15] = 255; kap[:, 1::2, 0] = 0
    th = 1008 * rng.integers(0, 2, (N, 8)); th[:, 0] = 0; th[:, 4] = 1008; th[:, 1::2] = 1008; th[0::2, 6] = 1008
    h[:, 1::2, :, T - 1] = 0; h[:, 1::2, 15, T - 1] = 63
    h[:, 6, :, T - 1] = 63; h[:, 0::4, :, T - 1] = 0
    few = rng.random((N, 8, T, 1)) < 0.7
    s1 = rng.integers(S, 16, (N, 8, T, 1)); s2 = S + (s1 - S + rng.integers(1, 16 - S, (N, 8, T, 1))) % (16 - S)
    nm = np.where(s == s1, 0, np.where(s == s2, PL - 1, (PL - 1) * rng.integers(0, 2, (N, 8, T, 16))))
    du = np.where(((s == s1) | (s == s2)) & (rng.random((N, 8, T, 16)) < 0.75), 0, FREE)
    nm = np.where(few, nm, p["nm"]); du = np.where(few, du, np.where((s >= S) & (rng.random((N, 8, T, 16)) < 0.6), 0, FREE))
    nm[:, 0::4, T - 1] = 0; du[:, 0::4, T - 1] = FREE
    u = (16 * 255 * 63) & 4095; e0 = ((u * u) >> 4) & (PL - 1); e1 = (((u * u) >> 4) + 255 * u) & (PL - 1)
    mem[e0 // C, 6, :, e0 % C] = 63; mem[e1 // C, 6, :, e1 % C] = 63
    nm[:, 6, T - 1] = e0; du[:, 6, T - 1] = FREE
    return pack({"mem": mem, "h": h, "val": val, "nm": nm, "du": du, "w": w, "kap": kap, "th": th})
def setup_inputs_meet(rng):
    p = parts(rng); b = np.array([0, 3, 4, 7]); e = np.array([1, 2, 5, 6]); gi = np.arange(8)[None, :, None]; s = np.arange(16)
    pool = p["nm"][0, :, 0].copy()
    nm = rng.permuted(np.broadcast_to(pool[None, :, None, :], (N, 8, T, 16)).copy(), axis=3); nm[:, 4] = pool[4]
    p["nm"][:, b] = nm[:, b]
    du = rng.integers(0, 3, (N, 8, T, 16)); dt = np.where(rng.random((N, 8, T, 16)) < 0.3, FREE, rng.integers(0, 2, (N, 8, T, 16)))
    du[:, e] = dt[:, e]; du[:, 4] = np.where((rng.random((N, T, 1)) < 0.2) & (s > S), FREE, 0); du[..., :S] = FREE; p["du"] = du
    pat = rng.integers(0, 4, (8, 6, 16)) * rng.choice(np.array([1, 3, 20]), (8, 1, 1))
    mem = pat[gi, rng.integers(0, 6, (N, 8, C))].transpose(0, 1, 3, 2)
    h = pat[gi, rng.integers(0, 6, (N, 8, T))].transpose(0, 1, 3, 2)
    val = pat[gi[..., None], rng.integers(0, 6, (N, 8, T, 16))].transpose(0, 1, 4, 2, 3)
    p["mem"][:, e] = mem[:, e]; p["h"][:, e] = h[:, e]; p["val"][:, e] = val[:, e]
    full = np.sum(np.max(pat, axis=1) - np.min(pat, axis=1), axis=1)
    off = rng.permuted(np.resize(np.array([0, 0, 1, -1, -3]), N * 4)).reshape(N, 4)
    p["th"][:, e] = np.maximum(full[e][None, :] + off, 0)
    p["th"][:, 0] = 0; p["th"][:, 4] = 0
    p["h"][:, 3] = p["h"][:1, 3, :, :1].copy(); p["w"][:, 3] = p["w"][:1, 3].copy(); p["kap"][:, 3] = p["kap"][:1, 3].copy()
    return pack(p)
def setup_inputs_spread(rng):
    p = parts(rng)
    p["mem"] = np.minimum((np.exp2(6 * rng.random((N, 8, 1, C))) * rng.random((N, 8, 16, C))).astype(np.int64), 63)
    p["h"] = np.minimum((np.exp2(6 * rng.random((N, 8, 1, T))) * rng.random((N, 8, 16, T))).astype(np.int64), 63)
    p["val"] = np.minimum((np.exp2(6 * rng.random((N, 8, 1, T, 16))) * rng.random((N, 8, 16, T, 16))).astype(np.int64), 63)
    p["w"] = np.minimum(np.exp2(8 * rng.random((N, 8, 16))).astype(np.int64), 255)
    p["th"] = rng.integers(0, 1009, (N, 8))
    du = np.where(rng.random((N, 8, T, 16)) < 0.5, rng.integers(0, 4, (N, 8, T, 16)), rng.integers(0, FREE + 1, (N, 8, T, 16))); du[..., :S] = FREE; p["du"] = du
    return pack(p)
def check_inputs(d):
    bad = []
    for k, lo, hi in RANGES:
        v = np.asarray(d[k]).astype(np.float64)
        if not (np.all(v >= lo) and np.all(v <= hi) and np.all(v == np.floor(v))): bad.append("range of " + k)
    du = np.asarray(d["due"]).astype(np.int64).reshape(N, 8, 16, T); nm = np.asarray(d["pnd"]).astype(np.int64).reshape(N, 8, 16, T)
    if np.any(du[:, :, :S] != FREE): bad.append("slots that start free")
    k = np.sort(np.where(du != FREE, nm, -1 - np.arange(16).reshape(1, 1, 16, 1)), axis=2)
    if np.any(k[:, :, 1:] == k[:, :, :-1]): bad.append("pending names of a thread differ")
    t = np.asarray(d["th"]).reshape(N, 8, 16)
    if np.any(t != t[:, :, :1]): bad.append("th alike in a group")
    return bad
def reference(mem, h, pnd, due, val, w, kap, th):
    whole = lambda a: a.astype(np.float32).astype(np.int64)
    mt = np.ascontiguousarray(whole(mem).reshape(N, 8, 16, C).transpose(1, 0, 3, 2)).reshape(8, PL, 16)
    hh = whole(h).reshape(N, 8, 16, T).transpose(0, 1, 3, 2)
    nm = pnd.astype(np.int64).reshape(N, 8, 16, T).transpose(0, 1, 3, 2).copy()
    du = due.astype(np.int64).reshape(N, 8, 16, T).transpose(0, 1, 3, 2).copy()
    vl = whole(val).reshape(N, 8, 16, T, 16).transpose(0, 1, 3, 4, 2).copy()
    ww = w.astype(np.int64).reshape(N, 8, 1, 16); kk = kap.astype(np.int64).reshape(N, 8, 1, 16); tt = th.astype(np.int64).reshape(N, 8, 16)[:, :, :1]
    A = np.zeros((N, 1, 1, 1), np.int64); s16 = np.arange(16); gi = np.arange(8).reshape(1, 8, 1, 1)
    for t in range(S):
        u = (np.sum(ww * hh, axis=3) & 4095)[..., None]
        z = ((u * u) >> 4) + kk * u + A
        a = np.where((s16 & 1) == 0, z, np.where(((z >> 3) & 1) == 1, nm + z, nm)) & (PL - 1)
        pend = du != FREE
        hit = (a[..., :, None] == nm[..., None, :]) & pend[..., None, :]
        x = np.where(np.any(hit, axis=4)[..., None], np.take_along_axis(vl, np.argmax(hit, axis=4)[..., None], 3), mt[gi, a])
        hi = np.max(x, axis=3); lo = np.min(x, axis=3); y = (hi + lo) >> 1
        score = np.sum(np.abs(x - hh[..., None, :]), axis=4)
        b = np.take_along_axis(a, np.argmax(score, axis=3)[..., None], 3)
        fence = np.sum(hi - lo, axis=3) >= tt
        same = (nm == b) & pend; had = np.any(same, axis=3)
        put = np.where(had[..., None], same, s16 == t) & ~fence[..., None]
        vl = np.where(put[..., None], y[..., None, :], vl); nm = np.where(put, b, nm)
        du[..., t] = np.where(~had & ~fence, t + 1 + (np.sum(y, axis=3) & DQ), du[..., t])
        sl = np.argmin(du, axis=3)[..., None]; least = np.take_along_axis(du, sl, 3)[..., 0]
        go = (least != FREE) & (fence | (least <= t))
        place = np.take_along_axis(nm, sl, 3)[..., 0]; value = np.take_along_axis(vl, sl[..., None], 3)[..., 0, :]
        du = np.where(go[..., None] & (s16 == sl), FREE, du)
        for g in range(8):
            m = go[:, g].reshape(-1); v = value[:, g].reshape(-1, 16)[m]
            first, at = np.unique(place[:, g].reshape(-1)[m], return_index=True)
            mt[g, first] = v[at]
        hh = np.abs(y - hh); A = (np.sum(fence, axis=(1, 2)) & 63).reshape(N, 1, 1, 1)
    bf = lambda e: np.ascontiguousarray(e).astype(np.float32).astype(BF)
    return {"ymem": bf(mt.reshape(8, N, C, 16).transpose(1, 0, 3, 2).reshape(N, 128, C)), "yh": bf(hh.transpose(0, 1, 3, 2).reshape(N, 128, T)),
            "ypnd": np.ascontiguousarray(nm.transpose(0, 1, 3, 2).reshape(N, 128, T)).astype(np.float32),
            "ydue": np.ascontiguousarray(du.transpose(0, 1, 3, 2).reshape(N, 128, T)).astype(np.float32),
            "yval": bf(vl.transpose(0, 1, 4, 2, 3).reshape(N, 128, 16 * T))}

@@ -1,0 +1,609 @@
+from concourse.bass import DstId, RemoteDMATransfer
+from concourse.mybir import AluOpType as A, AxisListType, ActivationFunctionType as AF
+
+VAL, TR, YB, END = 8192, 12288, 12544, 12800
+F31 = float(31 << 17)
+NSTEP = 4
+
+SCRATCH = {}
+
+
+def _d(where, dtype, **k):
+    for n, c in k.items():
+        SCRATCH[n] = (where, [128] + (list(c) if isinstance(c, (list, tuple)) else [c]), dtype)
+
+
+_d("sbuf", "bfloat16", win=END, hop=1024, d=4096, ab=4096, hrep=4096, hiS=4096, loS=4096, hiM=2048, loM=2048,
+   tmpv=4096, eq=4096, wI=2048, Eb=3072, Wb=128, Ab=128, G8=8, G16=16, Ib=128, n4I=128, n1I=128, onesb=128, cU=256, cN=256,
+   c129=128, KIa=256, KIb=256, CK2=256, TRI=128, hb=256, hm=256, Qb=256, HB=256, rng=256, sm=256, mb=256, gor=256,
+   fe16=16, oh=256, ohK=256, qA=1, dkap=128)
+for _t in range(NSTEP):
+    for _r in range(4):
+        _d("sbuf", "bfloat16", **{"rv%d_%d" % (_t, _r): 256})
+        _d("sbuf", "uint16", **{"rl%d_%d" % (_t, _r): 16})
+_d("sbuf", "float16", If=128, FT=512, LF=512, RF=512)
+_d("sbuf", "uint16", offN=256, ld=16, lst=16)
+_d("sbuf", "int32", wi=1, ki=1, thi=1, pni=256, dui=256, z=256, zb=128, zs=128, ai=256, mi=256, kmi=16, pl=16, sl=16, xi=48,
+   rb=32, Di=16, Dm=16, rci=16, fci=1, kei=256, key2=256)
+_d("sbuf", "float32", ones32=128, I32=128, t32=128, A32=128, M16=256, segM=256, segK=256, kapB=256, th16=16, iP=16, trP=16,
+   yP=16, trL=16, tl0=16, key=256, nm=256, Fm=256, nn=[16, 32], tA=256, tB=256, Acol=1, cA=1, Eo=256, offP=256,
+   kmf=256, kt=16, e1=16, e2=16, e3=16, R2=[48, 16], R3=[32, 16], dptM=256, d0=16, dsrc=16, dr=16, dy=16, sqx=48, n1=16, nq=16,
+   am=512, o1=16, offb=16, eqd=16, dyE=16, hv=16, a1=16, a2=16, a3=16, nf=16, r1=16, md=256, ms=256, gd=256, w3=256,
+   dk=16, nk=16, h0=16, fr=16, k1=16, k2=16, m1=16, m2=16, ft=16, sL=1, bL=1, sR=1, bR=1, s3=1, fcf=1, dth=128, of1=256,
+   wf=1, kf=1, tf=1, s13=1)
+PACK = {}
+
+
+def _pack(dtype, big):
+    at = 0
+    for n in [n for n, v in SCRATCH.items() if v[2] == dtype and len(v[1]) == 2 and v[1][1] <= 64]:
+        PACK[n] = (big, at, SCRATCH[n][1][1])
+        at += (SCRATCH[n][1][1] + 7) // 8 * 8
+        del SCRATCH[n]
+    SCRATCH[big] = ("sbuf", [128, at], dtype)
+
+
+_pack("float32", "pf")
+_pack("int32", "pi")
+for _b in range(8):
+    SCRATCH["ps%d" % _b] = ("psum", [128, 512], "float32")
+
+SEMAPHORES = ["vs", "ss", "pp", "gs", "loc", "locm", "marr", "hop0", "hop1", "hopl"]
+SEMAPHORES += ["dm%d" % i for i in range(24)]
+SEMAPHORES += [n + "%d_%d" % (t, r) for n in ("av", "al") for t in range(NSTEP) for r in range(4)]
+
+
+def relay_of(c, T, topo):
+    return [x for x in topo.cores_of(c) if topo.die(x) != topo.die(c)
+            and all(topo.may_write(x, y) for y in T.cores if y != c)][0]
+
+
+def send(g, T, topo, src, dsts, src_ap, dst_aps, sem, lsem):
+    ids, m = [], topo.mask(src, dsts[0])
+    for x in dsts:
+        rid, pid, _ = topo.addr(x)
+        ids.append(DstId(rid=rid, pnc=pid))
+        m &= topo.mask(src, x)
+    g.remote_dma_fused([RemoteDMATransfer(dst_ids=ids, dma_engine_mask=m, remote_sem=sem, srcs=[src_ap], dsts=dst_aps)], local_sem=lsem)
+    return bin(m).count("1")
+
+
+def relay(g, core, T, topo):
+    for r, c in enumerate(T.cores):
+        if relay_of(c, T, topo) == core:
+            oth = [x for x in T.cores if x != c]
+            n = 0
+            for j in range(2):
+                g.wait_ge(T.sem["hop%d" % j], bin(topo.mask(c, core)).count("1"))
+                lo = 2048 * r + 1024 + 512 * j
+                n += send(g, T, topo, core, oth, T.hop[:, 512 * j:512 * j + 512], [T.win[:, lo:lo + 512]] * 3, T.sem.marr, T.sem.hopl)
+            g.wait_ge(T.sem.hopl, n)
+
+
+def rank_program(g, core, T, topo):
+    rank = T.rank_of(core)
+    if rank is None:
+        relay(g, core, T, topo)
+        return
+    others = [x for x in T.cores if x != core]
+    ENG = {"v": (g.vector, "vs"), "s": (g.scalar, "ss"), "p": (g.tensor, "pp"), "g": (g, "gs"), "y": (g.sync, None)}
+    cnt = {"vs": 0, "ss": 0, "pp": 0, "gs": 0}
+    waited = {}
+    hist = {}
+    ndma = [0]
+    nloc = [0]
+
+    def X(n, lo=0, hi=None, st=1, p=None):
+        big, off, w = PACK[n] if n in PACK else (n, 0, None)
+        if w is None:
+            w = 512 if n[:2] == "ps" and n[2:].isdigit() else SCRATCH[n][1][1]
+        if hi is None:
+            hi = w
+        ap = T[big][:, off + lo:off + hi:st] if p is None else T[big][p[0]:p[1], off + lo:off + hi:st]
+        return (ap, big, off + lo, off + hi, st, (off + lo) % st, (off + lo) % st + 1)
+
+    def X3(n, s0, s1, a, b=None):
+        t = T[n]
+        w = SCRATCH[n][1][2]
+        ap = t[:, s0:s1, a] if b is None else t[:, s0:s1, a:b]
+        return (ap, n, s0 * w, s1 * w, w, a, a + 1 if b is None else b)
+
+    def IND(lo, hi, off):
+        return (T.win[:, lo:hi].indirect(off[0]), "win", lo, hi, 1, 0, 1)
+
+    def meet(e, f):
+        return e[0] < f[1] and f[0] < e[1] and (e[2] != f[2] or (e[3] < f[4] and f[3] < e[4]))
+
+    def wait(q, sem, val):
+        if waited.get((q, sem), 0) < val:
+            waited[(q, sem)] = val
+            ENG[q][0].wait_ge(T.sem[sem], val)
+
+    def need(q, rs, ws):
+        deps = {}
+        for regs, isw in ((rs, False), (ws, True)):
+            for x in regs:
+                b = x[1]
+                bank = b[:2] == "ps" and b[2:].isdigit()
+                for (r2, q2, sem, val, w2) in hist.get(b, []):
+                    if bank and q2 != q:
+                        hit = True
+                    else:
+                        hit = meet(x[2:], r2)
+                        if q2 == q:
+                            hit = hit and w2 and q != "p"
+                        else:
+                            hit = hit and (w2 or isw)
+                    if hit:
+                        deps[sem] = max(deps.get(sem, 0), val)
+        for sem, val in deps.items():
+            wait(q, sem, val)
+
+    def note(q, rs, ws, sem, val):
+        for regs, isw in ((rs, False), (ws, True)):
+            for x in regs:
+                h = hist.setdefault(x[1], [])
+                h[:] = [e for e in h if not (e[0] == x[2:] and e[1] == q and e[2] == sem and (isw or not e[4]))]
+                h.append((x[2:], q, sem, val, isw))
+
+    def op(q, rs, ws, fn):
+        need(q, rs, ws)
+        sem = ENG[q][1]
+        cnt[sem] += 1
+        fn(ENG[q][0]).then_inc(T.sem[sem], 1)
+        note(q, rs, ws, sem, cnt[sem])
+
+    def dma(q, out, in_, rs, ws):
+        need(q, rs, ws)
+        sem = "dm%d" % ndma[0]
+        ndma[0] += 1
+        ENG[q][0].dma_start(out, in_).then_inc(T.sem[sem], 16)
+        note(q + "d", rs, ws, sem, 16)
+
+    def cols(*xs):
+        return [x for x in xs if isinstance(x, tuple)]
+
+    def val_(x):
+        return x[0] if isinstance(x, tuple) else x
+
+    def tt(o, a, b, f, extra=()):
+        op("v", [a, b] + list(extra), [o], lambda e: e.tensor_tensor(o[0], a[0], b[0], f))
+
+    def ts(o, a, s1, f1, s2=None, f2=None):
+        if f2 is None:
+            op("v", [a] + cols(s1), [o], lambda e: e.tensor_scalar(o[0], a[0], val_(s1), None, f1))
+        else:
+            op("v", [a] + cols(s1, s2), [o], lambda e: e.tensor_scalar(o[0], a[0], val_(s1), val_(s2), f1, f2))
+
+    def cp(o, a, extra=()):
+        op("v", [a] + list(extra), [o], lambda e: e.tensor_copy(o[0], a[0]))
+
+    def ms(o, v):
+        op("v", [], [o], lambda e: e.memset(o[0], v))
+
+    def scan(o, a, b, ini, f1, f2):
+        op("v", [a, b], [o], lambda e: e.tensor_tensor_scan(o[0], a[0], b[0], ini, f1, f2))
+
+    def act(o, a, f, bias=0.0, scale=1.0):
+        op("s", [a] + cols(bias, scale), [o], lambda e: e.activation(o[0], a[0], f, bias=val_(bias), scale=val_(scale)))
+
+    def mm(o, l, r, start, stop):
+        op("p", [l, r], [o], lambda e: e.matmul(o[0], l[0], r[0], start, stop))
+
+    def tr(o, a, i):
+        op("p", [a, i], [o], lambda e: e.transpose(o[0], a[0], i[0]))
+
+    def iota(o, pat, base, cm):
+        op("g", [], [o], lambda e: e.iota(o[0], pat, base, cm, allow_small_or_imprecise_dtypes=True))
+
+    def asel(o, a, pat, cmp, fill, base, cm):
+        op("g", [a], [o], lambda e: e.affine_select(o[0], a[0], pat, cmp, fill, base, cm))
+
+    lo = 2048 * rank
+    own = [X("win", lo + 1024, lo + 1536), X("win", lo + 1536, lo + 2048), X("win", lo, lo + 1024)]
+    dma("y", own[0][0], T.mem[:, 1024:1536], [], [own[0]])
+    dma("s", own[1][0], T.mem[:, 1536:2048], [], [own[1]])
+    dma("y", own[2][0], T.mem[:, 0:1024], [], [own[2]])
+    for q, n, src in (("s", "pni", T.pnd), ("y", "dui", T.due), ("s", "hb", T.h), ("y", "wi", T.w), ("s", "ki", T.kap), ("y", "thi", T.th)):
+        dma(q, X(n)[0], src[:], [], [X(n)])
+    dma("s", X("tmpv")[0], T.val[:], [], [X("tmpv")])
+    ms(X("ones32"), 1.0)
+    asel(X("I32"), X("ones32"), [[-1, 128]], A.is_equal, 0.0, 0, 1)
+    rel = relay_of(core, T, topo)
+    nm_ = 0
+    for j in range(2):
+        need("g", [own[j]], [])
+        nm_ += send(g, T, topo, core, [rel], own[j][0], [T.hop[:, 512 * j:512 * j + 512]], T.sem["hop%d" % j], T.sem.locm)
+    need("g", [own[2]], [])
+    nm_ += send(g, T, topo, core, others, own[2][0], [own[2][0]] * 3, T.sem.marr, T.sem.locm)
+    arr = 0
+    for x in others:
+        y = relay_of(x, T, topo)
+        arr += bin(topo.mask(x, core)).count("1") + 2 * bin(topo.mask(y, core)).count("1")
+    for r in range(4):
+        hist.setdefault("win", []).append(((2048 * r, 2048 * r + 2048, 1, 0, 1), "x") + (("locm", nm_, False) if r == rank else ("marr", arr, True)))
+
+    asel(X("t32"), X("ones32"), [[-16, 8], [0, 16]], A.is_ge, 0.0, 0, 1)
+    asel(X("A32"), X("t32"), [[16, 8], [0, 16]], A.is_ge, 0.0, 15, -1)
+    iota(X("mi"), [[0, 16], [-1, 16]], 16, 1)
+    iota(X("iP"), [[128, 2], [0, 8]], 0, 1)
+    iota(X("KIa"), [[128, 2], [0, 8], [256, 16]], -8192, 0)
+    iota(X("KIb"), [[0, 256]], 0, 1)
+    iota(X("CK2"), [[0, 16], [-128, 16]], 1920, 0)
+    iota(X("rci"), [[0, 16]], 0, 1)
+    iota(X("tl0"), [[16, 16]], TR, 0)
+    iota(X("fci"), [[0, 1]], 0, 1)
+    asel(X("dth"), X("ones32"), [[-1, 128]], A.is_ge, 0.0, 0, 1)
+    cp(X("wf"), X("wi"))
+    cp(X("Ib"), X("I32"))
+    cp(X("Ab"), X("A32"))
+    ts(X("Wb"), X("A32"), X("wf"), A.mult)
+    ms(X("onesb"), 1.0)
+    ms(X("cU"), 4128.0)
+    ts(X("n4I"), X("Ib"), -4096.0, A.mult)
+    cp(X("kf"), X("ki"))
+    ts(X("dkap"), X("Ib"), X("kf"), A.mult)
+    for hf in range(2):
+        mm(X("ps2", 128 * hf, 128 * hf + 128), X("onesb"), X("dkap"), True, True)
+    cp(X("kapB"), X("ps2", 0, 256))
+    ts(X("rci"), X("rci"), 15, A.bitwise_and)
+    ts(X("s13"), X("rci", 0, 1), 8192.0, A.mult)
+    ts(X("key"), X("dui"), 131072.0, A.mult, X("s13"), A.add)
+    tt(X("offP"), X("key"), X("pni"), A.add)
+    cp(X("Fm"), X("pni"))
+    for hf in range(2):
+        s = (128 * hf, 128 * hf + 128)
+        tr(X("ps3", *s), X("offP", *s), X("I32"))
+        tr(X("ps3", s[0] + 256, s[1] + 256), X("Fm", *s), X("I32"))
+    cp(X("key"), X("ps3", 0, 256))
+    cp(X("nm"), X("ps3", 256, 512))
+    cp(X("tf"), X("thi"))
+    cp(X("TRI"), X("dth"))
+    ts(X("t32"), X("I32"), X("tf"), A.mult)
+    for hf in range(2):
+        mm(X("ps2", 128 * hf, 128 * hf + 128), X("ones32"), X("t32"), True, True)
+    cp(X("th16"), X("ps2", 0, 256, 16))
+    ms(X("Acol"), -8256.0)
+    for r in range(16):
+        if r % 2:
+            ts(X("wI", 128 * r, 128 * r + 128), X("Ib"), 256.0 * (64 + r), A.mult)
+        else:
+            act(X("wI", 128 * r, 128 * r + 128), X("Ib"), AF.Copy, scale=256.0 * (64 + r))
+    act(X("hm"), X("hb"), AF.Copy, bias=-192.0)
+    ts(X("mi"), X("mi"), 15, A.bitwise_and)
+    ts(X("M16"), X("mi"), 0.0, A.is_equal)
+    cp(X("ps3", 256, 512), X("M16"))
+    ts(X("trP"), X("iP"), float(TR), A.add)
+    ts(X("yP"), X("iP"), float(YB), A.add)
+    tt(X("trL"), X("tl0"), X("rci"), A.add)
+    ts(X("n1I"), X("Ib"), -128.0, A.mult)
+    cp(X("If"), X("I32"))
+    cp(X("G8"), X("Ab", 0, 128, 16))
+    ts(X("G16", 0, 8), X("G8"), 2048.0, A.mult)
+    ts(X("G16", 8, 16), X("G8"), 2048.0, A.mult)
+    ms(X("c129"), 129.0)
+    ms(X("cN"), -128.0)
+    ms(X("segM"), 1.0)
+    ms(X("segM", 0, 256, 16), 0.0)
+    ms(X("segK"), 0.0)
+    ms(X("segK", 0, 256, 16), 16777216.0)
+    ms(X("hiM"), 200.0)
+    ms(X("hiM", 0, 2048, 16), -200.0)
+    ms(X("loM"), -200.0)
+    ms(X("loM", 0, 2048, 16), 200.0)
+    ms(X("win", TR, END), 0.0)
+    ts(X("fci"), X("fci"), 31, A.bitwise_and)
+    cp(X("fcf"), X("fci"))
+    ts(X("sL"), X("fcf"), 4.0, A.is_lt)
+    ts(X("bL"), X("fcf"), 4.0, A.is_equal)
+    ts(X("s3"), X("fcf"), 3.0, A.is_lt, -2.0, A.mult)
+    tt(X("sR"), X("s3"), X("bL"), A.add)
+    ts(X("bR"), X("fcf"), 3.0, A.is_equal)
+    ms(X("of1"), 0.0)
+    for j in range(2):
+        cp(X("FT", 256 * j, 256 * j + 256), X("of1"))
+
+    def double(n, s0, s1):
+        for a in (1, 2, 4, 8):
+            cp(X3(n, s0, s1, a, 2 * a), X3(n, s0, s1, 0, a))
+
+    def hash_pe():
+        for hf in range(2):
+            s = (128 * hf, 128 * hf + 128)
+            mm(X("ps0", *s), X("hb", *s), X("Wb"), True, True)
+        mm(X("ps1", 0, 256), X("onesb"), X("cU"), True, False)
+        for hf in range(2):
+            s = (128 * hf, 128 * hf + 128)
+            mm(X("ps1", *s), X("hb", *s), X("Wb"), False, False)
+
+    def hash_q():
+        ts(X("Qb"), X("ps0", 0, 256), 1.0 / 4096, A.mult, 128.5 + 2.0 ** -13, A.add)
+        mm(X("ps1", 0, 256), X("n4I"), X("Qb"), False, True)
+
+    def names():
+        ts(X("Fm"), X("key"), F31, A.is_ge, 16384.0, A.mult)
+        tt(X3("nn", 0, 16, 0, 16), X("Fm"), X("nm"), A.add)
+
+    def places():
+        tt(X("tB"), X("ps1", 0, 256), X("kapB"), A.mult)
+        act(X("ps1", 0, 256), X("ps1", 0, 256), AF.Square, scale=0.25)
+        ts(X("tA"), X("tB"), X("Acol"), A.add, 8255.75, A.add)
+
+    def places2():
+        tt(X("z"), X("ps1", 0, 256), X("tA"), A.add)
+        ts(X("zb"), X("z", 1, 256, 2), 3, A.logical_shift_right, 1, A.bitwise_and)
+        tt(X("zs"), X("zb"), X("z", 1, 256, 2), A.mult)
+        tt(X("z", 1, 256, 2), X("zs"), X("nm", 1, 256, 2), A.add)
+        ts(X("ai"), X("z"), 8191, A.bitwise_and)
+        cp(X("ps3", 0, 256), X("ai"))
+
+    def hits():
+        mm(X("ps2", 0, 256), X("Ib"), X("KIa"), True, False)
+        mm(X("ps2", 0, 256), X("Ib"), X("KIb"), False, False)
+        for r in range(16):
+            e = X("eq", 256 * r, 256 * r + 256)
+            tt(e, X("ps3", 0, 256), X3("nn", 0, 16, r, r + 16), A.is_equal)
+            mm(X("ps2", 0, 256), X("wI", 128 * r, 128 * r + 128), e, False, r == 15)
+
+    def offsets():
+        ts(X("Eo"), X("ps2", 0, 256), 12288.0, A.is_ge, -4096.0, A.mult)
+        tt(X("Eo"), X("ps2", 0, 256), X("Eo"), A.add)
+        tt(X("offP"), X("ps3", 0, 256), X("Eo"), A.max)
+        for hf in range(2):
+            s = (128 * hf, 128 * hf + 128)
+            tr(X("ps7", *s), X("offP", *s), X("I32"))
+        cp(X("offN"), X("ps7", 0, 256))
+        act(X("HB"), X("offP"), AF.Copy, bias=128.5 + 1.0 / 256, scale=1.0 / 128)
+        for hf in range(2):
+            s = (128 * hf, 128 * hf + 128)
+            b = "ps%d" % (4 + hf)
+            mm(X(b, 0, 256), X("Ib"), X("CK2"), True, False)
+            mm(X(b, 0, 128), X("I32"), X("offP", *s), False, False)
+            mm(X(b, 0, 128), X("onesb"), X("c129"), False, False)
+            mm(X(b, 0, 128), X("n1I"), X("HB", *s), False, False)
+            mm(X(b, 128, 256), X("Ib"), X("HB", *s), False, False)
+
+    def hreps():
+        for k in range(16):
+            act(X("hrep", k, 4096, 16), X("hb"), AF.Copy)
+
+    def drainer(t):
+        scan(X("kmf"), X("segK"), X("key"), 0.0, A.max, A.min)
+        k15 = X("kmf", 15, 256, 16)
+        cp(X("kmi"), k15)
+        cp(X3("R2", 0, 16, 0), k15)
+        ts(X("e1"), k15, F31, A.is_ge, 4096.0, A.mult)
+        ts(X("e2"), k15, float((t + 1) << 17), A.is_lt, -8192.0, A.mult)
+        ts(X("pl"), X("kmi"), 8191, A.bitwise_and)
+        ts(X("sl"), X("kmi"), 13, A.logical_shift_right, 15, A.bitwise_and)
+        tt(X("e3"), X("e1"), X("e2"), A.add)
+        ts(X("xi", 0, 16), X("pl"), 8, A.logical_shift_right, 31, A.bitwise_and)
+        ts(X("xi", 16, 32), X("pl"), 4, A.logical_shift_right, 15, A.bitwise_and)
+        ts(X("xi", 32, 48), X("pl"), 15, A.bitwise_and)
+        tt(X3("R2", 16, 32, 0), X("e3"), X("th16"), A.add)
+        tt(X3("R2", 32, 48, 0), X("pl"), X("trP"), A.subtract)
+        ts(X("d0"), X("sl"), 256.0, A.mult, float(VAL), A.add)
+        tt(X("sqx"), X("xi"), X("xi"), A.mult)
+        cp(X3("R2", 0, 48, 1, 2), X3("R2", 0, 48, 0, 1))
+        tt(X("dsrc"), X("d0"), X("iP"), A.add)
+        tt(X("n1"), X("sqx", 0, 16), X("sqx", 16, 32), A.add)
+        for f in range(3):
+            cp(X("FT", f, 512, 32), X("xi", 16 * f, 16 * f + 16))
+        cp(X3("R2", 0, 48, 2, 4), X3("R2", 0, 48, 0, 2))
+        tt(X("nq"), X("n1"), X("sqx", 32, 48), A.add)
+        tt(X("dr"), X("dsrc"), X("trP"), A.subtract)
+        tt(X("dy"), X("yP"), X("dsrc"), A.subtract)
+        cp(X3("R2", 0, 48, 4, 8), X3("R2", 0, 48, 0, 4))
+        cp(X("FT", 3, 512, 32), X("nq"))
+        cp(X("FT", 4, 512, 32), X("nq"))
+        cp(X3("R2", 0, 48, 8, 16), X3("R2", 0, 48, 0, 8))
+        tt(X("oh"), X("key"), X3("R2", 0, 16, 0, 16), A.is_equal)
+        tt(X("dptM"), X("ps3", 256, 512), X3("R2", 32, 48, 0, 16), A.mult)
+        ts(X("ohK"), X("oh"), 4194304.0, A.mult)
+
+    def same_pe():
+        for j in range(4):
+            mm(X("ps6", 128 * j, 128 * j + 128), X("FT", 128 * j, 128 * j + 128), X("If"), True, True)
+        act(X("LF"), X("ps6"), AF.Identity, bias=X("bL"), scale=X("sL"))
+        act(X("RF"), X("ps6"), AF.Identity, bias=X("bR"), scale=X("sR"))
+
+    def same(gr):
+        q, st = gr % 4, gr // 4
+        b = "ps%d" % (6 + gr % 2)
+        p = (32 * q, 32 * q + 5)
+        b0, b1 = (128 * st, 128 * st + 128), (256 + 128 * st, 384 + 128 * st)
+        mm(X(b, 0, 128), X("LF", *b0, p=p), X("RF", *b0, p=p), True, False)
+        mm(X(b, 0, 128), X("Ib"), X("TRI"), False, True)
+        mm(X(b, 128, 256), X("LF", *b0, p=p), X("RF", *b1, p=p), True, True)
+        mm(X(b, 256, 384), X("LF", *b1, p=p), X("RF", *b1, p=p), True, False)
+        mm(X(b, 256, 384), X("Ib"), X("TRI"), False, True)
+        act(X("Eb", 384 * gr, 384 * gr + 384), X(b, 0, 384), AF.Relu, bias=16384.0, scale=-16384.0)
+
+    def gather(hf):
+        o = X("d", 2048 * hf, 2048 * hf + 2048)
+        f = X("offN", 128 * hf, 128 * hf + 128)
+        tt(o, IND(0, TR, f), X("hrep", 2048 * hf, 2048 * hf + 2048), A.subtract, extra=[f])
+        act(X("ab", 2048 * hf, 2048 * hf + 2048), o, AF.Abs)
+        b = "ps%d" % (4 + hf)
+        for k in range(16):
+            mm(X(b, k, 256, 16), X("ab", 2048 * hf + k, 2048 * hf + 2048, 16), X("G16"), False, k == 15)
+
+    def hi(hf):
+        s = (2048 * hf, 2048 * hf + 2048)
+        scan(X("hiS", *s), X("hiM"), X("d", *s), -200.0, A.min, A.max)
+
+    def lo_(hf):
+        s = (2048 * hf, 2048 * hf + 2048)
+        scan(X("loS", *s), X("loM"), X("d", *s), 200.0, A.max, A.min)
+
+    def rs(hf):
+        s = (2048 * hf + 15, 2048 * hf + 2048, 16)
+        o = (128 * hf, 128 * hf + 128)
+        tt(X("rng", *o), X("hiS", *s), X("loS", *s), A.subtract)
+        mm(X("ps0", *o), X("rng", *o), X("Ab"), True, True)
+        tt(X("sm", *o), X("hiS", *s), X("loS", *s), A.add)
+
+    def amax(hf):
+        scan(X("am", 256 * hf, 256 * hf + 256), X("segM"), X("ps%d" % (4 + hf), 0, 256), 0.0, A.mult, A.max)
+
+    def lconv(bank, c, src):
+        for hf in range(2):
+            mm(X(bank, c + 8 * hf, c + 8 * hf + 8), X(src, 128 * hf, 128 * hf + 128), X("A32", 0, 128, 16), True, False)
+            mm(X(bank, c + 8 * hf, c + 8 * hf + 8), X("I32"), X("trL", 8 * hf, 8 * hf + 8), False, True)
+
+    hash_pe()
+    hash_q()
+    names()
+    places()
+    act(X3("nn", 0, 16, 16, 32), X3("nn", 0, 16, 0, 16), AF.Copy)
+    for s in range(0, 16, 2):
+        act(X("win", VAL + 256 * s, VAL + 256 * s + 256), X("tmpv", s, 4096, 16), AF.Copy)
+    hreps()
+    places2()
+    hits()
+    for s in range(1, 16, 2):
+        cp(X("win", VAL + 256 * s, VAL + 256 * s + 256), X("tmpv", s, 4096, 16))
+    offsets()
+    drainer(0)
+    same_pe()
+    for gr in range(8):
+        same(gr)
+
+    for t in range(NSTEP):
+        last = t == NSTEP - 1
+        gather(0)
+        gather(1)
+        hi(0)
+        lo_(0)
+        rs(0)
+        amax(0)
+        hi(1)
+        ts(X("mb", 0, 128), X("sm", 0, 128), 0.5, A.mult, 191.75, A.add)
+        amax(1)
+        ts(X("ft"), X("iP"), float(VAL + 256 * t), A.add)
+        lo_(1)
+        for hf in range(2):
+            cp(X("rb", 16 * hf, 16 * hf + 16), X("am", 256 * hf + 15, 256 * hf + 256, 16))
+        rs(1)
+        ts(X("rb"), X("rb"), 127, A.bitwise_and)
+        ts(X("mb", 128, 256), X("sm", 128, 256), 0.5, A.mult, 191.75, A.add)
+        for hf in range(2):
+            ts(X("o1", 8 * hf, 8 * hf + 8), X("rb", 16 * hf + 8, 16 * hf + 16), 128.0, A.mult, -128.0, A.add)
+        tt(X("win", YB, END), X("mb"), X("hm"), A.add)
+        for hf in range(2):
+            tt(X("offb", 8 * hf, 8 * hf + 8), X("o1", 8 * hf, 8 * hf + 8), X("rb", 16 * hf, 16 * hf + 8), A.add)
+        mm(X("ps1", 0, 256), X("onesb"), X("cN"), True, False)
+        tt(X("gor"), X("ps0", 0, 256), X3("R2", 16, 32, 0, 16), A.is_ge)
+        for gr in range(8):
+            for hf in range(2):
+                o = X("ps1", 128 * hf + 16 * gr, 128 * hf + 16 * gr + 16)
+                e = 384 * gr
+                mm(o, X("Eb", e + 128 * hf, e + 128 * hf + 128), X("gor", 16 * gr, 16 * gr + 16), False, False)
+                if hf:
+                    mm(o, X("Eb", e + 256, e + 384), X("gor", 128 + 16 * gr, 144 + 16 * gr), False, gr == 7)
+        tt(X("eqd"), X("offb"), X("dsrc"), A.is_equal)
+        tt(X("nf"), X("ps0", 0, 256, 16), X("th16"), A.is_lt)
+        tt(X("a1"), X("offb"), X("ft"), A.subtract)
+        ts(X("hv"), X("offb"), float(VAL), A.is_ge)
+        tt(X("dyE"), X("eqd"), X("dy"), A.mult)
+        tt(X("fe16"), X("ps0", 0, 256, 16), X("th16"), A.is_ge)
+        tt(X("a2"), X("hv"), X("a1"), A.mult)
+        tt(X("r1"), X("dyE"), X("nf"), A.mult)
+        ts(X("a3"), X("a2"), float(VAL + 256 * t - TR), A.add)
+        tt(X3("R3", 0, 16, 0), X("r1"), X("dr"), A.add)
+        tt(X3("R3", 16, 32, 0), X("a3"), X("nf"), A.mult)
+        double("R3", 0, 32)
+        tt(X("md"), X("ps3", 256, 512), X3("R3", 0, 16, 0, 16), A.mult)
+        lconv("ps2", 256, "md")
+        tt(X("gd"), X("gor"), X("dptM"), A.mult)
+        tt(X("ms"), X("ps3", 256, 512), X3("R3", 16, 32, 0, 16), A.mult)
+        cp(X("ld"), X("ps2", 256, 272))
+        lconv("ps7", 400, "ms")
+        for hf in range(2):
+            mm(X("ps6", 400 + 8 * hf, 408 + 8 * hf), X("win", YB + 128 * hf, YB + 128 * hf + 128), X("G8"), True, True)
+        mm(X("ps6", 416, 432), X("onesb"), X("fe16"), True, True)
+        dv = X("rv%d_%d" % (t, rank))
+        cp(dv, IND(0, END, X("ld")), extra=[X("ld")])
+        need("g", [dv], [])
+        nloc[0] += send(g, T, topo, core, others, dv[0], [dv[0]] * 3, T.sem["av%d_%d" % (t, rank)], T.sem.loc)
+        tt(X("w3"), X("ps1", 0, 256), X("gd"), A.max)
+        ts(X("w3"), X("w3"), 0.0, A.min)
+        lconv("ps1", 256, "w3")
+        cp(X("lst"), X("ps7", 400, 416))
+        ls = X("rl%d_%d" % (t, rank))
+        cp(ls, X("ps1", 256, 272))
+        need("g", [ls], [])
+        nloc[0] += send(g, T, topo, core, others, ls[0], [ls[0]] * 3, T.sem["al%d_%d" % (t, rank)], T.sem.loc)
+        ts(X("hm"), X("mb"), -192.0, A.add)
+        act(X("hb"), X("hm"), AF.Abs)
+        if not last:
+            hash_pe()
+            act(X("hm"), X("hb"), AF.Copy, bias=-192.0)
+        cp(IND(0, YB, X("lst")), X("win", YB, END), extra=[X("lst")])
+        tt(X("oh"), X("ohK"), X("gor"), A.mult)
+        cp(X("Di"), X("ps6", 400, 416))
+        if not last:
+            op("v", [X("ps6", 416, 432)], [X("cA")], lambda e: e.tensor_reduce(X("cA")[0], X("ps6", 416, 432)[0], AxisListType.X, A.add))
+        tt(X("key"), X("key"), X("oh"), A.add)
+        ts(X("Dm"), X("Di"), 3, A.bitwise_and)
+        ts(X("h0"), X("offb"), float(VAL), A.is_lt)
+        if not last:
+            ts(X("qA"), X("cA"), 1.0 / 64, A.mult, 128.5 + 1.0 / 128, A.add)
+        ts(X("dk"), X("Dm"), 131072.0, A.mult, float(((t + 1) << 17) + (t << 13)), A.add)
+        tt(X("fr"), X("h0"), X("nf"), A.mult)
+        tt(X("m1"), X("offb"), X("nm", t, 256, 16), A.subtract)
+        if not last:
+            ts(X("Acol"), X("qA"), -64.0, A.mult, X("cA"), A.add)
+            hash_q()
+        tt(X("nk"), X("dk"), X("offb"), A.add)
+        tt(X("m2"), X("m1"), X("fr"), A.mult)
+        tt(X("k1"), X("nk"), X("key", t, 256, 16), A.subtract)
+        tt(X("nm", t, 256, 16), X("m2"), X("nm", t, 256, 16), A.add)
+        tt(X("k2"), X("k1"), X("fr"), A.mult)
+        tt(X("key", t, 256, 16), X("k2"), X("key", t, 256, 16), A.add)
+        if not last:
+            places()
+            names()
+            act(X3("nn", 0, 16, 16, 32), X3("nn", 0, 16, 0, 16), AF.Copy)
+            hreps()
+            places2()
+            hits()
+            offsets()
+            drainer(t + 1)
+            same_pe()
+            for gr in range(8):
+                same(gr)
+        else:
+            for s in range(16):
+                o, i = X("tmpv", s, 4096, 16), X("win", VAL + 256 * s, VAL + 256 * s + 256)
+                if s % 2:
+                    cp(o, i)
+                else:
+                    act(o, i, AF.Copy)
+            dma("y", T.yval[:], X("tmpv")[0], [X("tmpv")], [])
+            dma("y", T.yh[:], X("hb")[0], [X("hb")], [])
+            cp(X("kei"), X("key"))
+            ts(X("key2"), X("kei"), 17, A.logical_shift_right)
+            ts(X("of1"), X("key2"), 31.0, A.min)
+            for hf in range(2):
+                s = (128 * hf, 128 * hf + 128)
+                tr(X("ps4", *s), X("of1", *s), X("I32"))
+                tr(X("ps5", *s), X("nm", *s), X("I32"))
+            act(X("tA"), X("ps4", 0, 256), AF.Copy)
+            act(X("tB"), X("ps5", 0, 256), AF.Copy)
+            dma("y", T.ydue[:], X("tA")[0], [X("tA")], [])
+            dma("y", T.ypnd[:], X("tB")[0], [X("tB")], [])
+        for r in range(len(T.cores) - 1, -1, -1):
+            if r != rank:
+                n = bin(topo.mask(T.cores[r], core)).count("1")
+                wait("v", "av%d_%d" % (t, r), n)
+                wait("v", "al%d_%d" % (t, r), n)
+            sv, sl = X("rv%d_%d" % (t, r)), X("rl%d_%d" % (t, r))
+            cp(IND(0, YB, sl), sv, extra=[sl])
+    o = X("win", lo, lo + 2048)
+    dma("y", T.ymem[:], o[0], [o], [])
+    for q in ("vs", "ss", "pp", "gs"):
+        wait("g", q, cnt[q])
+    wait("g", "loc", nloc[0])
+    for j in range(ndma[0]):
+        wait("g", "dm%d" % j, 16)

@@ -4,7 +4,9 @@ from concourse.mybir import AluOpType as A, AxisListType, ActivationFunctionType
 VAL, TR, YB, END = 8192, 12288, 12544, 12800
 F31 = float(31 << 17)
 NSTEP = 4
-
+SH = 64
+NS1 = 8
+HV = 9
 SCRATCH = {}
 
 
@@ -14,9 +16,9 @@ def _d(where, dtype, **k):
 
 
 _d("sbuf", "bfloat16", win=END, hop=1024, d=4096, ab=4096, hrep=4096, hiS=4096, loS=4096, hiM=2048, loM=2048,
-   tmpv=4096, eq=4096, wI=2048, Eb=3072, Wb=128, Ab=128, G8=8, G16=16, Ib=128, n4I=128, n1I=128, onesb=128, cU=256, cN=256,
-   c129=128, KIa=256, KIb=256, CK2=256, TRI=128, hb=256, hm=256, Qb=256, HB=256, rng=256, sm=256, mb=256, gor=256,
-   fe16=16, oh=256, ohK=256, qA=1, dkap=128)
+   tmpv=4096, eq=4096, wI=2048, Eb=3072, Wb=128, Ab=128, nAb=128, G8=8, G16=16, Ib=128, n4I=128, n1I=128, nI=128, nEI=128,
+   nBI=128, onesb=128, cU=256, KIa=256, KIb=256, CK2=256, tLa=16, tLb=16, hb=256, hm=256, Qb=256, HB=256, mb=256, gor=256,
+   fe16=16, qA=1, dkap=128)
 for _t in range(NSTEP):
     for _r in range(4):
         _d("sbuf", "bfloat16", **{"rv%d_%d" % (_t, _r): 256})
@@ -24,12 +26,12 @@ for _t in range(NSTEP):
 _d("sbuf", "float16", If=128, FT=512, LF=512, RF=512)
 _d("sbuf", "uint16", offN=256, ld=16, lst=16)
 _d("sbuf", "int32", wi=1, ki=1, thi=1, pni=256, dui=256, z=256, zb=128, zs=128, ai=256, mi=256, kmi=16, pl=16, sl=16, xi=48,
-   rb=32, Di=16, Dm=16, rci=16, fci=1, kei=256, key2=256)
-_d("sbuf", "float32", ones32=128, I32=128, t32=128, A32=128, M16=256, segM=256, segK=256, kapB=256, th16=16, iP=16, trP=16,
-   yP=16, trL=16, tl0=16, key=256, nm=256, Fm=256, nn=[16, 32], tA=256, tB=256, Acol=1, cA=1, Eo=256, offP=256,
-   kmf=256, kt=16, e1=16, e2=16, e3=16, R2=[48, 16], R3=[32, 16], dptM=256, d0=16, dsrc=16, dr=16, dy=16, sqx=48, n1=16, nq=16,
-   am=512, o1=16, offb=16, eqd=16, dyE=16, hv=16, a1=16, a2=16, a3=16, nf=16, r1=16, md=256, ms=256, gd=256, w3=256,
-   dk=16, nk=16, h0=16, fr=16, k1=16, k2=16, m1=16, m2=16, ft=16, sL=1, bL=1, sR=1, bR=1, s3=1, fcf=1, dth=128, of1=256,
+   rb=32, Di=16, Dm=16, rci=16, fci=1)
+_d("sbuf", "float32", ones32=128, I32=128, t32=128, A32=128, segM=256, segK=256, kapB=256, th16=16, iP=16, trP=16,
+   yP=16, tl0=16, key=256, nm=256, nn=[16, 32], tA=256, tB=256, Acol=1, cA=1, Eo=256, offP=256,
+   kmf=256, e1=16, e2=16, e3=16, R2=[48, 16], R3=[32, 16], dptM=256, d0=16, dsrc=16, dr=16, dy=16, sqx=48, n1=16, nq=16,
+   am=512, o1=16, offb=16, eqd=16, dyE=16, hv=16, a1=16, a2=16, a3=16, nf=16, r1=16, md=256, ms=256, w3=256,
+   dk=16, nk=16, h0=16, fr=16, k1=16, k2=16, m1=16, m2=16, ft=16, sL=1, bL=1, sR=1, bR=1, s3=1, fcf=1,
    wf=1, kf=1, tf=1, s13=1)
 PACK = {}
 
@@ -58,6 +60,10 @@ def relay_of(c, T, topo):
             and all(topo.may_write(x, y) for y in T.cores if y != c)][0]
 
 
+def width(m):
+    return bin(m).count("1")
+
+
 def send(g, T, topo, src, dsts, src_ap, dst_aps, sem, lsem):
     ids, m = [], topo.mask(src, dsts[0])
     for x in dsts:
@@ -65,7 +71,7 @@ def send(g, T, topo, src, dsts, src_ap, dst_aps, sem, lsem):
         ids.append(DstId(rid=rid, pnc=pid))
         m &= topo.mask(src, x)
     g.remote_dma_fused([RemoteDMATransfer(dst_ids=ids, dma_engine_mask=m, remote_sem=sem, srcs=[src_ap], dsts=dst_aps)], local_sem=lsem)
-    return bin(m).count("1")
+    return width(m)
 
 
 def relay(g, core, T, topo):
@@ -74,7 +80,7 @@ def relay(g, core, T, topo):
             oth = [x for x in T.cores if x != c]
             n = 0
             for j in range(2):
-                g.wait_ge(T.sem["hop%d" % j], bin(topo.mask(c, core)).count("1"))
+                g.wait_ge(T.sem["hop%d" % j], width(topo.mask(c, core)))
                 lo = 2048 * r + 1024 + 512 * j
                 n += send(g, T, topo, core, oth, T.hop[:, 512 * j:512 * j + 512], [T.win[:, lo:lo + 512]] * 3, T.sem.marr, T.sem.hopl)
             g.wait_ge(T.sem.hopl, n)
@@ -184,8 +190,8 @@ def rank_program(g, core, T, topo):
     def scan(o, a, b, ini, f1, f2):
         op("v", [a, b], [o], lambda e: e.tensor_tensor_scan(o[0], a[0], b[0], ini, f1, f2))
 
-    def act(o, a, f, bias=0.0, scale=1.0):
-        op("s", [a] + cols(bias, scale), [o], lambda e: e.activation(o[0], a[0], f, bias=val_(bias), scale=val_(scale)))
+    def act(o, a, f, bias=0.0, scale=1.0, extra=()):
+        op("s", [a] + cols(bias, scale) + list(extra), [o], lambda e: e.activation(o[0], a[0], f, bias=val_(bias), scale=val_(scale)))
 
     def mm(o, l, r, start, stop):
         op("p", [l, r], [o], lambda e: e.matmul(o[0], l[0], r[0], start, stop))
@@ -204,11 +210,17 @@ def rank_program(g, core, T, topo):
     dma("y", own[0][0], T.mem[:, 1024:1536], [], [own[0]])
     dma("s", own[1][0], T.mem[:, 1536:2048], [], [own[1]])
     dma("y", own[2][0], T.mem[:, 0:1024], [], [own[2]])
-    for q, n, src in (("s", "pni", T.pnd), ("y", "dui", T.due), ("s", "hb", T.h), ("y", "wi", T.w), ("s", "ki", T.kap), ("y", "thi", T.th)):
+    for q, n, src in (("s", "wi", T.w), ("y", "pni", T.pnd), ("s", "hb", T.h), ("y", "dui", T.due), ("s", "ki", T.kap), ("y", "thi", T.th)):
         dma(q, X(n)[0], src[:], [], [X(n)])
     dma("s", X("tmpv")[0], T.val[:], [], [X("tmpv")])
     ms(X("ones32"), 1.0)
     asel(X("I32"), X("ones32"), [[-1, 128]], A.is_equal, 0.0, 0, 1)
+    asel(X("t32"), X("ones32"), [[-16, 8], [0, 16]], A.is_ge, 0.0, 0, 1)
+    asel(X("A32"), X("t32"), [[16, 8], [0, 16]], A.is_ge, 0.0, 15, -1)
+    iota(X("rci"), [[0, 16]], 0, 1)
+    iota(X("iP"), [[128, 2], [0, 8]], 0, 1)
+    iota(X("fci"), [[0, 1]], 0, 1)
+    iota(X("mi"), [[0, 16], [-1, 16]], 16, 1)
     rel = relay_of(core, T, topo)
     nm_ = 0
     for j in range(2):
@@ -219,187 +231,115 @@ def rank_program(g, core, T, topo):
     arr = 0
     for x in others:
         y = relay_of(x, T, topo)
-        arr += bin(topo.mask(x, core)).count("1") + 2 * bin(topo.mask(y, core)).count("1")
+        arr += width(topo.mask(x, core)) + 2 * width(topo.mask(y, core))
     for r in range(4):
         hist.setdefault("win", []).append(((2048 * r, 2048 * r + 2048, 1, 0, 1), "x") + (("locm", nm_, False) if r == rank else ("marr", arr, True)))
-
-    asel(X("t32"), X("ones32"), [[-16, 8], [0, 16]], A.is_ge, 0.0, 0, 1)
-    asel(X("A32"), X("t32"), [[16, 8], [0, 16]], A.is_ge, 0.0, 15, -1)
-    iota(X("mi"), [[0, 16], [-1, 16]], 16, 1)
-    iota(X("iP"), [[128, 2], [0, 8]], 0, 1)
     iota(X("KIa"), [[128, 2], [0, 8], [256, 16]], -8192, 0)
     iota(X("KIb"), [[0, 256]], 0, 1)
-    iota(X("CK2"), [[0, 16], [-128, 16]], 1920, 0)
-    iota(X("rci"), [[0, 16]], 0, 1)
-    iota(X("tl0"), [[16, 16]], TR, 0)
-    iota(X("fci"), [[0, 1]], 0, 1)
-    asel(X("dth"), X("ones32"), [[-1, 128]], A.is_ge, 0.0, 0, 1)
-    cp(X("wf"), X("wi"))
-    cp(X("Ib"), X("I32"))
-    cp(X("Ab"), X("A32"))
-    ts(X("Wb"), X("A32"), X("wf"), A.mult)
+    iota(X("CK2"), [[-16512, 2], [0, 8], [-128, 16]], 18432, 0)
+    iota(X("tl0"), [[16, 16]], 0, 0)
+
     ms(X("onesb"), 1.0)
     ms(X("cU"), 4128.0)
+    ms(X("segK"), 0.0)
+    ms(X("segK", 0, 256, 16), 16777216.0)
+    cp(X("Ib"), X("I32"))
     ts(X("n4I"), X("Ib"), -4096.0, A.mult)
+    cp(X("wf"), X("wi"))
+    ts(X("Wb"), X("A32"), X("wf"), A.mult)
+    ts(X("rci"), X("rci"), 15, A.bitwise_and)
+    ts(X("s13"), X("rci", 0, 1), 8192.0, A.mult)
     cp(X("kf"), X("ki"))
     ts(X("dkap"), X("Ib"), X("kf"), A.mult)
     for hf in range(2):
         mm(X("ps2", 128 * hf, 128 * hf + 128), X("onesb"), X("dkap"), True, True)
-    cp(X("kapB"), X("ps2", 0, 256))
-    ts(X("rci"), X("rci"), 15, A.bitwise_and)
-    ts(X("s13"), X("rci", 0, 1), 8192.0, A.mult)
+    cp(X("tA"), X("pni"))
     ts(X("key"), X("dui"), 131072.0, A.mult, X("s13"), A.add)
-    tt(X("offP"), X("key"), X("pni"), A.add)
-    cp(X("Fm"), X("pni"))
+    tt(X("offP"), X("key"), X("tA"), A.add)
     for hf in range(2):
         s = (128 * hf, 128 * hf + 128)
+        tr(X("ps3", s[0] + 256, s[1] + 256), X("tA", *s), X("I32"))
         tr(X("ps3", *s), X("offP", *s), X("I32"))
-        tr(X("ps3", s[0] + 256, s[1] + 256), X("Fm", *s), X("I32"))
-    cp(X("key"), X("ps3", 0, 256))
-    cp(X("nm"), X("ps3", 256, 512))
+    act(X("kapB"), X("ps2", 0, 256), AF.Copy)
     cp(X("tf"), X("thi"))
-    cp(X("TRI"), X("dth"))
     ts(X("t32"), X("I32"), X("tf"), A.mult)
+    cp(X("nm"), X("ps3", 256, 512))
+    cp(X("key"), X("ps3", 0, 256))
     for hf in range(2):
         mm(X("ps2", 128 * hf, 128 * hf + 128), X("ones32"), X("t32"), True, True)
-    cp(X("th16"), X("ps2", 0, 256, 16))
-    ms(X("Acol"), -8256.0)
+    ms(X("Acol"), -0.25)
     for r in range(16):
-        if r % 2:
-            ts(X("wI", 128 * r, 128 * r + 128), X("Ib"), 256.0 * (64 + r), A.mult)
-        else:
-            act(X("wI", 128 * r, 128 * r + 128), X("Ib"), AF.Copy, scale=256.0 * (64 + r))
+        act(X("wI", 128 * r, 128 * r + 128), X("Ib"), AF.Copy, scale=256.0 * (64 + r))
     act(X("hm"), X("hb"), AF.Copy, bias=-192.0)
-    ts(X("mi"), X("mi"), 15, A.bitwise_and)
-    ts(X("M16"), X("mi"), 0.0, A.is_equal)
-    cp(X("ps3", 256, 512), X("M16"))
-    ts(X("trP"), X("iP"), float(TR), A.add)
-    ts(X("yP"), X("iP"), float(YB), A.add)
-    tt(X("trL"), X("tl0"), X("rci"), A.add)
-    ts(X("n1I"), X("Ib"), -128.0, A.mult)
-    cp(X("If"), X("I32"))
-    cp(X("G8"), X("Ab", 0, 128, 16))
-    ts(X("G16", 0, 8), X("G8"), 2048.0, A.mult)
-    ts(X("G16", 8, 16), X("G8"), 2048.0, A.mult)
-    ms(X("c129"), 129.0)
-    ms(X("cN"), -128.0)
-    ms(X("segM"), 1.0)
-    ms(X("segM", 0, 256, 16), 0.0)
-    ms(X("segK"), 0.0)
-    ms(X("segK", 0, 256, 16), 16777216.0)
-    ms(X("hiM"), 200.0)
-    ms(X("hiM", 0, 2048, 16), -200.0)
-    ms(X("loM"), -200.0)
-    ms(X("loM", 0, 2048, 16), 200.0)
-    ms(X("win", TR, END), 0.0)
-    ts(X("fci"), X("fci"), 31, A.bitwise_and)
-    cp(X("fcf"), X("fci"))
-    ts(X("sL"), X("fcf"), 4.0, A.is_lt)
-    ts(X("bL"), X("fcf"), 4.0, A.is_equal)
-    ts(X("s3"), X("fcf"), 3.0, A.is_lt, -2.0, A.mult)
-    tt(X("sR"), X("s3"), X("bL"), A.add)
-    ts(X("bR"), X("fcf"), 3.0, A.is_equal)
-    ms(X("of1"), 0.0)
-    for j in range(2):
-        cp(X("FT", 256 * j, 256 * j + 256), X("of1"))
 
-    def double(n, s0, s1):
+    def double_s(n, s0, s1):
         for a in (1, 2, 4, 8):
-            cp(X3(n, s0, s1, a, 2 * a), X3(n, s0, s1, 0, a))
+            act(X3(n, s0, s1, a, 2 * a), X3(n, s0, s1, 0, a), AF.Copy)
+
+    def halves():
+        return [(hf, (128 * hf, 128 * hf + 128)) for hf in range(2)]
 
     def hash_pe():
-        for hf in range(2):
-            s = (128 * hf, 128 * hf + 128)
+        for hf, s in halves():
             mm(X("ps0", *s), X("hb", *s), X("Wb"), True, True)
         mm(X("ps1", 0, 256), X("onesb"), X("cU"), True, False)
-        for hf in range(2):
-            s = (128 * hf, 128 * hf + 128)
+        for hf, s in halves():
             mm(X("ps1", *s), X("hb", *s), X("Wb"), False, False)
-
-    def hash_q():
-        ts(X("Qb"), X("ps0", 0, 256), 1.0 / 4096, A.mult, 128.5 + 2.0 ** -13, A.add)
+        act(X("Qb"), X("ps0", 0, 256), AF.Copy, bias=128.5 + 2.0 ** -13, scale=1.0 / 4096)
         mm(X("ps1", 0, 256), X("n4I"), X("Qb"), False, True)
 
     def names():
-        ts(X("Fm"), X("key"), F31, A.is_ge, 16384.0, A.mult)
-        tt(X3("nn", 0, 16, 0, 16), X("Fm"), X("nm"), A.add)
+        act(X("ps0", 256, 512), X("key"), AF.Relu, bias=(1 - F31) * 16384.0, scale=16384.0)
+        act(X("ps5", 256, 512), X("key"), AF.Copy)
 
-    def places():
-        tt(X("tB"), X("ps1", 0, 256), X("kapB"), A.mult)
-        act(X("ps1", 0, 256), X("ps1", 0, 256), AF.Square, scale=0.25)
-        ts(X("tA"), X("tB"), X("Acol"), A.add, 8255.75, A.add)
-
-    def places2():
-        tt(X("z"), X("ps1", 0, 256), X("tA"), A.add)
-        ts(X("zb"), X("z", 1, 256, 2), 3, A.logical_shift_right, 1, A.bitwise_and)
-        tt(X("zs"), X("zb"), X("z", 1, 256, 2), A.mult)
-        tt(X("z", 1, 256, 2), X("zs"), X("nm", 1, 256, 2), A.add)
-        ts(X("ai"), X("z"), 8191, A.bitwise_and)
-        cp(X("ps3", 0, 256), X("ai"))
-
-    def hits():
-        mm(X("ps2", 0, 256), X("Ib"), X("KIa"), True, False)
-        mm(X("ps2", 0, 256), X("Ib"), X("KIb"), False, False)
-        for r in range(16):
-            e = X("eq", 256 * r, 256 * r + 256)
-            tt(e, X("ps3", 0, 256), X3("nn", 0, 16, r, r + 16), A.is_equal)
-            mm(X("ps2", 0, 256), X("wI", 128 * r, 128 * r + 128), e, False, r == 15)
-
-    def offsets():
-        ts(X("Eo"), X("ps2", 0, 256), 12288.0, A.is_ge, -4096.0, A.mult)
-        tt(X("Eo"), X("ps2", 0, 256), X("Eo"), A.add)
-        tt(X("offP"), X("ps3", 0, 256), X("Eo"), A.max)
-        for hf in range(2):
-            s = (128 * hf, 128 * hf + 128)
-            tr(X("ps7", *s), X("offP", *s), X("I32"))
-        cp(X("offN"), X("ps7", 0, 256))
-        act(X("HB"), X("offP"), AF.Copy, bias=128.5 + 1.0 / 256, scale=1.0 / 128)
-        for hf in range(2):
-            s = (128 * hf, 128 * hf + 128)
-            b = "ps%d" % (4 + hf)
-            mm(X(b, 0, 256), X("Ib"), X("CK2"), True, False)
-            mm(X(b, 0, 128), X("I32"), X("offP", *s), False, False)
-            mm(X(b, 0, 128), X("onesb"), X("c129"), False, False)
-            mm(X(b, 0, 128), X("n1I"), X("HB", *s), False, False)
-            mm(X(b, 128, 256), X("Ib"), X("HB", *s), False, False)
-
-    def hreps():
-        for k in range(16):
-            act(X("hrep", k, 4096, 16), X("hb"), AF.Copy)
+    def names2():
+        tt(X3("nn", 0, 16, 0, 16), X("ps0", 256, 512), X("nm"), A.add)
+        act(X3("nn", 0, 16, 16, 32), X3("nn", 0, 16, 0, 16), AF.Copy)
 
     def drainer(t):
         scan(X("kmf"), X("segK"), X("key"), 0.0, A.max, A.min)
         k15 = X("kmf", 15, 256, 16)
+        yield
         cp(X("kmi"), k15)
-        cp(X3("R2", 0, 16, 0), k15)
         ts(X("e1"), k15, F31, A.is_ge, 4096.0, A.mult)
         ts(X("e2"), k15, float((t + 1) << 17), A.is_lt, -8192.0, A.mult)
+        cp(X3("R2", 0, 16, 0), k15)
+        yield
         ts(X("pl"), X("kmi"), 8191, A.bitwise_and)
         ts(X("sl"), X("kmi"), 13, A.logical_shift_right, 15, A.bitwise_and)
         tt(X("e3"), X("e1"), X("e2"), A.add)
+        yield
+        tt(X3("R2", 32, 48, 0), X("pl"), X("trP"), A.subtract)
         ts(X("xi", 0, 16), X("pl"), 8, A.logical_shift_right, 31, A.bitwise_and)
+        tt(X3("R2", 16, 32, 0), X("e3"), X("th16"), A.add)
+        double_s("R2", 0, 48)
+        yield
         ts(X("xi", 16, 32), X("pl"), 4, A.logical_shift_right, 15, A.bitwise_and)
         ts(X("xi", 32, 48), X("pl"), 15, A.bitwise_and)
-        tt(X3("R2", 16, 32, 0), X("e3"), X("th16"), A.add)
-        tt(X3("R2", 32, 48, 0), X("pl"), X("trP"), A.subtract)
         ts(X("d0"), X("sl"), 256.0, A.mult, float(VAL), A.add)
+        yield
         tt(X("sqx"), X("xi"), X("xi"), A.mult)
-        cp(X3("R2", 0, 48, 1, 2), X3("R2", 0, 48, 0, 1))
         tt(X("dsrc"), X("d0"), X("iP"), A.add)
+        cp(X("FT", 0, 512, 32), X("xi", 0, 16))
+        yield
         tt(X("n1"), X("sqx", 0, 16), X("sqx", 16, 32), A.add)
-        for f in range(3):
-            cp(X("FT", f, 512, 32), X("xi", 16 * f, 16 * f + 16))
-        cp(X3("R2", 0, 48, 2, 4), X3("R2", 0, 48, 0, 2))
+        cp(X("FT", 1, 512, 32), X("xi", 16, 32))
+        cp(X("FT", 2, 512, 32), X("xi", 32, 48))
+        yield
         tt(X("nq"), X("n1"), X("sqx", 32, 48), A.add)
         tt(X("dr"), X("dsrc"), X("trP"), A.subtract)
         tt(X("dy"), X("yP"), X("dsrc"), A.subtract)
-        cp(X3("R2", 0, 48, 4, 8), X3("R2", 0, 48, 0, 4))
-        cp(X("FT", 3, 512, 32), X("nq"))
-        cp(X("FT", 4, 512, 32), X("nq"))
-        cp(X3("R2", 0, 48, 8, 16), X3("R2", 0, 48, 0, 8))
-        tt(X("oh"), X("key"), X3("R2", 0, 16, 0, 16), A.is_equal)
+        act(X("FT", 3, 512, 32), X("nq"), AF.Copy)
+        act(X("FT", 4, 512, 32), X("nq"), AF.Copy)
+        same_pe()
+        yield
+
+    def drainer2():
         tt(X("dptM"), X("ps3", 256, 512), X3("R2", 32, 48, 0, 16), A.mult)
-        ts(X("ohK"), X("oh"), 4194304.0, A.mult)
+
+    def drainer3():
+        tt(X("ps4", 256, 512), X("ps5", 256, 512), X3("R2", 0, 16, 0, 16), A.is_equal)
+        act(X("ps4", 256, 512), X("ps4", 256, 512), AF.Copy, scale=4194304.0)
 
     def same_pe():
         for j in range(4):
@@ -412,21 +352,90 @@ def rank_program(g, core, T, topo):
         b = "ps%d" % (6 + gr % 2)
         p = (32 * q, 32 * q + 5)
         b0, b1 = (128 * st, 128 * st + 128), (256 + 128 * st, 384 + 128 * st)
-        mm(X(b, 0, 128), X("LF", *b0, p=p), X("RF", *b0, p=p), True, False)
-        mm(X(b, 0, 128), X("Ib"), X("TRI"), False, True)
-        mm(X(b, 128, 256), X("LF", *b0, p=p), X("RF", *b1, p=p), True, True)
-        mm(X(b, 256, 384), X("LF", *b1, p=p), X("RF", *b1, p=p), True, False)
-        mm(X(b, 256, 384), X("Ib"), X("TRI"), False, True)
+        mm(X(b, 0, 128), X("LF", *b0, p=p), X("RF", *b0, p=p), True, True)
+        mm(X(b, 128, 256), X("LF", *b1, p=p), X("RF", *b1, p=p), True, True)
+        mm(X(b, 256, 384), X("LF", *b0, p=p), X("RF", *b1, p=p), True, True)
         act(X("Eb", 384 * gr, 384 * gr + 384), X(b, 0, 384), AF.Relu, bias=16384.0, scale=-16384.0)
+        e = X("Eb", 384 * gr, 384 * gr + 256)
+        asel(e, e, [[0, 2], [1, 128]], A.is_gt, 0.0, 0, -1)
 
-    def gather(hf):
-        o = X("d", 2048 * hf, 2048 * hf + 2048)
-        f = X("offN", 128 * hf, 128 * hf + 128)
-        tt(o, IND(0, TR, f), X("hrep", 2048 * hf, 2048 * hf + 2048), A.subtract, extra=[f])
-        act(X("ab", 2048 * hf, 2048 * hf + 2048), o, AF.Abs)
-        b = "ps%d" % (4 + hf)
-        for k in range(16):
-            mm(X(b, k, 256, 16), X("ab", 2048 * hf + k, 2048 * hf + 2048, 16), X("G16"), False, k == 15)
+    def address(fill, first):
+        mm(X("ps2", 0, 256), X("Ib"), X("KIa"), True, False)
+        mm(X("ps2", 0, 256), X("Ib"), X("KIb"), False, False)
+        tt(X("tB"), X("ps1", 0, 256), X("kapB"), A.mult)
+        act(X("ps1", 0, 256), X("ps1", 0, 256), AF.Square, scale=0.25)
+        act(X("tA"), X("tB"), AF.Identity, bias=X("Acol"))
+        fill(1)
+        names2()
+        fill(2)
+        tt(X("z"), X("ps1", 0, 256), X("tA"), A.add)
+        fill(1)
+        ts(X("zb"), X("z", 1, 256, 2), 3, A.logical_shift_right, 1, A.bitwise_and)
+        fill(1)
+        tt(X("zs"), X("zb"), X("z", 1, 256, 2), A.mult)
+        fill(1)
+        tt(X("z", 1, 256, 2), X("zs"), X("nm", 1, 256, 2), A.add)
+        fill(1)
+        ts(X("ai"), X("z"), 8191, A.bitwise_and)
+        fill(1)
+        cp(X("ps3", 0, 256), X("ai"))
+        fill(9)
+        if first:
+            hrep("s", 0, 11)
+        for r in range(16):
+            e = X("eq", 256 * r, 256 * r + 256)
+            tt(e, X("ps3", 0, 256), X3("nn", 0, 16, r, r + 16), A.is_equal)
+            mm(X("ps2", 0, 256), X("wI", 128 * r, 128 * r + 128), e, False, r == 15)
+        if first:
+            hrep("s", 11, 16)
+        drainer2()
+        drainer3()
+        if not first:
+            hrep("v", HV, 12)
+        ts(X("Eo"), X("ps2", 0, 256), 12288.0, A.is_ge, -4096.0, A.mult)
+        if not first:
+            hrep("v", 12, 13)
+        tt(X("Eo"), X("Eo"), X("ps2", 0, 256), A.add)
+
+    def offsets(first):
+        if not first:
+            hrep("v", 13, 14)
+        tt(X("offP"), X("Eo"), X("ps3", 0, 256), A.max)
+        if not first:
+            hrep("v", 14, 16)
+        for hf, s in halves():
+            tr(X("ps7", *s), X("offP", *s), X("I32"))
+        act(X("HB"), X("offP"), AF.Copy, bias=128.5 + 1.0 / 256, scale=1.0 / 128)
+
+    def offsets2():
+        cp(X("offN"), X("ps7", 0, 256))
+        for hf, s in halves():
+            b = "ps%d" % (4 + hf)
+            mm(X(b, 0, 256), X("Ib"), X("CK2"), True, False)
+            mm(X(b, 0, 128), X("I32"), X("offP", *s), False, False)
+            mm(X(b, 0, 128), X("n1I"), X("HB", *s), False, False)
+            mm(X(b, 128, 256), X("Ib"), X("HB", *s), False, False)
+        for gr in range(NS1):
+            same(gr)
+
+    def hrep(q, a, b):
+        for k in range(a, b):
+            if q == "v":
+                cp(X("hrep", k, 4096, 16), X("hb"))
+            else:
+                act(X("hrep", k, 4096, 16), X("hb"), AF.Copy)
+
+    def lconv(bank, c, src):
+        mm(X(bank, c, c + 16), X("Ib"), X("tLa"), True, False)
+        mm(X(bank, c, c + 16), X("Ib"), X("tLb"), False, False)
+        for hf, s in halves():
+            mm(X(bank, c + 8 * hf, c + 8 * hf + 8), X(src, *s), X("A32", 0, 128, 16), False, hf == 1)
+
+    def filler(gen):
+        def fill(n):
+            for _ in range(n):
+                next(gen, None)
+        return fill
 
     def hi(hf):
         s = (2048 * hf, 2048 * hf + 2048)
@@ -436,166 +445,199 @@ def rank_program(g, core, T, topo):
         s = (2048 * hf, 2048 * hf + 2048)
         scan(X("loS", *s), X("loM"), X("d", *s), 200.0, A.max, A.min)
 
-    def rs(hf):
-        s = (2048 * hf + 15, 2048 * hf + 2048, 16)
-        o = (128 * hf, 128 * hf + 128)
-        tt(X("rng", *o), X("hiS", *s), X("loS", *s), A.subtract)
-        mm(X("ps0", *o), X("rng", *o), X("Ab"), True, True)
-        tt(X("sm", *o), X("hiS", *s), X("loS", *s), A.add)
-
     def amax(hf):
         scan(X("am", 256 * hf, 256 * hf + 256), X("segM"), X("ps%d" % (4 + hf), 0, 256), 0.0, A.mult, A.max)
 
-    def lconv(bank, c, src):
-        for hf in range(2):
-            mm(X(bank, c + 8 * hf, c + 8 * hf + 8), X(src, 128 * hf, 128 * hf + 128), X("A32", 0, 128, 16), True, False)
-            mm(X(bank, c + 8 * hf, c + 8 * hf + 8), X("I32"), X("trL", 8 * hf, 8 * hf + 8), False, True)
+    def score(hf):
+        b = "ps%d" % (4 + hf)
+        for k in range(16):
+            mm(X(b, k, 256, 16), X("ab", 2048 * hf + k, 2048 * hf + 2048, 16), X("G16"), False, k == 15)
 
     hash_pe()
-    hash_q()
     names()
-    places()
-    act(X3("nn", 0, 16, 16, 32), X3("nn", 0, 16, 0, 16), AF.Copy)
-    for s in range(0, 16, 2):
-        act(X("win", VAL + 256 * s, VAL + 256 * s + 256), X("tmpv", s, 4096, 16), AF.Copy)
-    hreps()
-    places2()
-    hits()
-    for s in range(1, 16, 2):
+    cp(X("th16"), X("ps2", 0, 256, 16))
+    ts(X("trP"), X("iP"), float(TR), A.add)
+    ts(X("yP"), X("iP"), float(YB), A.add)
+    ts(X("fci"), X("fci"), 31, A.bitwise_and)
+    ms(X("dptM"), 0.0)
+    cp(X("fcf"), X("fci"))
+    cp(X("FT", 0, 256), X("dptM"))
+    cp(X("FT", 256, 512), X("dptM"))
+    ts(X("sL"), X("fcf"), 4.0, A.is_lt)
+    ts(X("bL"), X("fcf"), 4.0, A.is_equal)
+    ts(X("s3"), X("fcf"), 3.0, A.is_lt, -2.0, A.mult)
+    ts(X("bR"), X("fcf"), 3.0, A.is_equal)
+    tt(X("sR"), X("s3"), X("bL"), A.add)
+    cp(X("If"), X("I32"))
+    ts(X("mi"), X("mi"), 15, A.bitwise_and)
+    ts(X("ps3", 256, 512), X("mi"), 0.0, A.is_equal)
+    address(filler(drainer(0)), True)
+    ts(X("n1I"), X("Ib"), -128.0, A.mult)
+    ts(X("G16", 0, 8), X("A32", 0, 128, 16), 2048.0, A.mult)
+    ts(X("G16", 8, 16), X("A32", 0, 128, 16), 2048.0, A.mult)
+    offsets(True)
+    for s in range(0, 16):
         cp(X("win", VAL + 256 * s, VAL + 256 * s + 256), X("tmpv", s, 4096, 16))
-    offsets()
-    drainer(0)
-    same_pe()
-    for gr in range(8):
-        same(gr)
+    offsets2()
+    ts(X("nI"), X("Ib"), -1.0, A.mult)
+    ts(X("nBI"), X("Ib"), -2.0, A.mult)
+    ts(X("nEI"), X("Ib"), -16384.0, A.mult)
+    cp(X("Ab"), X("A32"))
+    ts(X("nAb"), X("A32"), -1.0, A.mult)
+    cp(X("G8"), X("A32", 0, 128, 16))
+    tt(X("tLb"), X("tl0"), X("rci"), A.add)
+    ms(X("tLa"), float(TR))
+    ms(X("segM"), 1.0)
+    ms(X("segM", 0, 256, 16), 0.0)
+    ms(X("hiM"), 200.0)
+    ms(X("hiM", 0, 2048, 16), -200.0)
+    ms(X("loM"), -200.0)
+    ms(X("loM", 0, 2048, 16), 200.0)
+    ms(X("win", TR, END), 0.0)
 
     for t in range(NSTEP):
         last = t == NSTEP - 1
-        gather(0)
-        gather(1)
+        c1, f1 = 4096 - 16 * SH, 256 - SH
+        fs = X("offN", f1, 256)
+        act(X("d", c1, 4096), IND(0, TR, fs), AF.Copy, extra=[fs])
+        for a, e in ((0, 128), (128, f1)):
+            fv, o = X("offN", a, e), X("d", 16 * a, 16 * e)
+            tt(o, IND(0, TR, fv), X("hrep", 16 * a, 16 * e), A.subtract, extra=[fv])
+        bl = [("ps2", c1), ("ps1", c1 + 512), ("ps0", c1 + 1024)][:SH // 32]
+        for b, c in bl:
+            mm(X(b), X("nI"), X("hrep", c, c + 512), True, False)
+            mm(X(b), X("Ib"), X("d", c, c + 512), False, True)
+        act(X("ab", 0, 2048), X("d", 0, 2048), AF.Abs)
+        score(0)
+        act(X("ab", 2048, c1), X("d", 2048, c1), AF.Abs)
+        for b, c in bl:
+            act(X("ab", c, c + 512), X(b), AF.Abs)
+        score(1)
+        for gr in range(NS1, 8):
+            same(gr)
         hi(0)
         lo_(0)
-        rs(0)
-        amax(0)
+        for hf, s in halves()[:1]:
+            mm(X("ps0", *s), X("hiS", 15, 2048, 16), X("Ab"), True, False)
+            mm(X("ps0", *s), X("loS", 15, 2048, 16), X("nAb"), False, True)
         hi(1)
-        ts(X("mb", 0, 128), X("sm", 0, 128), 0.5, A.mult, 191.75, A.add)
-        amax(1)
+        amax(0)
         ts(X("ft"), X("iP"), float(VAL + 256 * t), A.add)
         lo_(1)
+        s = (128, 256)
+        mm(X("ps0", *s), X("hiS", 2063, 4096, 16), X("Ab"), True, False)
+        mm(X("ps0", *s), X("loS", 2063, 4096, 16), X("nAb"), False, True)
+        mm(X("ps7", 0, 256), X("Ib"), X("hiS", 15, 4096, 16), True, False)
+        mm(X("ps7", 0, 256), X("Ib"), X("loS", 15, 4096, 16), False, False)
+        mm(X("ps7", f1, 256), X("nBI"), X("hb", f1, 256), False, True)
+        amax(1)
+        act(X("mb"), X("ps7", 0, 256), AF.Copy, bias=191.75, scale=0.5)
+        mm(X("ps6", 0, 256), X("Ib"), X("mb"), True, False)
+        mm(X("ps6", 0, 256), X("Ib"), X("hm"), False, True)
+        act(X("hb"), X("mb"), AF.Abs, bias=-192.0)
         for hf in range(2):
             cp(X("rb", 16 * hf, 16 * hf + 16), X("am", 256 * hf + 15, 256 * hf + 256, 16))
-        rs(1)
-        ts(X("rb"), X("rb"), 127, A.bitwise_and)
-        ts(X("mb", 128, 256), X("sm", 128, 256), 0.5, A.mult, 191.75, A.add)
-        for hf in range(2):
-            ts(X("o1", 8 * hf, 8 * hf + 8), X("rb", 16 * hf + 8, 16 * hf + 16), 128.0, A.mult, -128.0, A.add)
-        tt(X("win", YB, END), X("mb"), X("hm"), A.add)
-        for hf in range(2):
-            tt(X("offb", 8 * hf, 8 * hf + 8), X("o1", 8 * hf, 8 * hf + 8), X("rb", 16 * hf, 16 * hf + 8), A.add)
-        mm(X("ps1", 0, 256), X("onesb"), X("cN"), True, False)
         tt(X("gor"), X("ps0", 0, 256), X3("R2", 16, 32, 0, 16), A.is_ge)
+        mm(X("ps1", 0, 256), X("nEI"), X("gor"), True, False)
         for gr in range(8):
             for hf in range(2):
                 o = X("ps1", 128 * hf + 16 * gr, 128 * hf + 16 * gr + 16)
                 e = 384 * gr
-                mm(o, X("Eb", e + 128 * hf, e + 128 * hf + 128), X("gor", 16 * gr, 16 * gr + 16), False, False)
+                mm(o, X("Eb", e + 256 * hf, e + 256 * hf + 128), X("gor", 16 * gr, 16 * gr + 16), False, False)
                 if hf:
-                    mm(o, X("Eb", e + 256, e + 384), X("gor", 128 + 16 * gr, 144 + 16 * gr), False, gr == 7)
-        tt(X("eqd"), X("offb"), X("dsrc"), A.is_equal)
+                    mm(o, X("Eb", e + 128, e + 256), X("gor", 128 + 16 * gr, 144 + 16 * gr), False, gr == 7)
+        act(X("win", YB, END), X("ps6", 0, 256), AF.Copy)
+        ts(X("rb"), X("rb"), 127, A.bitwise_and)
         tt(X("nf"), X("ps0", 0, 256, 16), X("th16"), A.is_lt)
+        for hf in range(2):
+            ts(X("o1", 8 * hf, 8 * hf + 8), X("rb", 16 * hf + 8, 16 * hf + 16), 128.0, A.mult, -128.0, A.add)
+        tt(X("fe16"), X("ps0", 0, 256, 16), X("th16"), A.is_ge)
+        for hf in range(2):
+            tt(X("offb", 8 * hf, 8 * hf + 8), X("o1", 8 * hf, 8 * hf + 8), X("rb", 16 * hf, 16 * hf + 8), A.add)
+        tt(X("ps4", 256, 512), X("ps4", 256, 512), X("gor"), A.mult)
+        tt(X("eqd"), X("offb"), X("dsrc"), A.is_equal)
         tt(X("a1"), X("offb"), X("ft"), A.subtract)
         ts(X("hv"), X("offb"), float(VAL), A.is_ge)
+        ts(X("h0"), X("offb"), float(VAL), A.is_lt)
         tt(X("dyE"), X("eqd"), X("dy"), A.mult)
-        tt(X("fe16"), X("ps0", 0, 256, 16), X("th16"), A.is_ge)
+        tt(X("m1"), X("offb"), X("nm", t, 256, 16), A.subtract)
         tt(X("a2"), X("hv"), X("a1"), A.mult)
         tt(X("r1"), X("dyE"), X("nf"), A.mult)
+        tt(X("fr"), X("h0"), X("nf"), A.mult)
         ts(X("a3"), X("a2"), float(VAL + 256 * t - TR), A.add)
         tt(X3("R3", 0, 16, 0), X("r1"), X("dr"), A.add)
+        tt(X("m2"), X("m1"), X("fr"), A.mult)
         tt(X3("R3", 16, 32, 0), X("a3"), X("nf"), A.mult)
-        double("R3", 0, 32)
-        tt(X("md"), X("ps3", 256, 512), X3("R3", 0, 16, 0, 16), A.mult)
-        lconv("ps2", 256, "md")
-        tt(X("gd"), X("gor"), X("dptM"), A.mult)
-        tt(X("ms"), X("ps3", 256, 512), X3("R3", 16, 32, 0, 16), A.mult)
-        cp(X("ld"), X("ps2", 256, 272))
-        lconv("ps7", 400, "ms")
+        double_s("R3", 0, 32)
+        act(X("ps1", 0, 256), X("ps1", 0, 256), AF.Relu, scale=-1.0 / 16384)
         for hf in range(2):
             mm(X("ps6", 400 + 8 * hf, 408 + 8 * hf), X("win", YB + 128 * hf, YB + 128 * hf + 128), X("G8"), True, True)
         mm(X("ps6", 416, 432), X("onesb"), X("fe16"), True, True)
+        tt(X("key"), X("key"), X("ps4", 256, 512), A.add)
+        tt(X("nm", t, 256, 16), X("m2"), X("nm", t, 256, 16), A.add)
+        if not last:
+            hrep("v", 0, HV)
+        cp(X("Di"), X("ps6", 400, 416))
+        if not last:
+            op("v", [X("ps6", 416, 432)], [X("cA")], lambda e: e.tensor_reduce(X("cA")[0], X("ps6", 416, 432)[0], AxisListType.X, A.add))
+        tt(X("k1"), X("key", t, 256, 16), X("offb"), A.subtract)
+        ts(X("Dm"), X("Di"), 3, A.bitwise_and)
+        if not last:
+            ts(X("qA"), X("cA"), 1.0 / 64, A.mult, 128.5 + 1.0 / 128, A.add)
+            ts(X("cA"), X("cA"), 8255.75, A.add)
+        ts(X("dk"), X("Dm"), 131072.0, A.mult, float(((t + 1) << 17) + (t << 13)), A.add)
+        tt(X("w3"), X("ps1", 0, 256), X("dptM"), A.mult)
+        tt(X("md"), X("ps3", 256, 512), X3("R3", 0, 16, 0, 16), A.mult)
+        lconv("ps2", 256, "md")
+        lconv("ps1", 256, "w3")
+        tt(X("ms"), X("ps3", 256, 512), X3("R3", 16, 32, 0, 16), A.mult)
+        lconv("ps7", 400, "ms")
+        tt(X("k2"), X("dk"), X("k1"), A.subtract)
+        if not last:
+            ts(X("Acol"), X("qA"), -64.0, A.mult, X("cA"), A.add)
+        tt(X("k2"), X("k2"), X("fr"), A.mult)
+        cp(X("ld"), X("ps2", 256, 272))
+        tt(X("key", t, 256, 16), X("k2"), X("key", t, 256, 16), A.add)
         dv = X("rv%d_%d" % (t, rank))
         cp(dv, IND(0, END, X("ld")), extra=[X("ld")])
         need("g", [dv], [])
         nloc[0] += send(g, T, topo, core, others, dv[0], [dv[0]] * 3, T.sem["av%d_%d" % (t, rank)], T.sem.loc)
-        tt(X("w3"), X("ps1", 0, 256), X("gd"), A.max)
-        ts(X("w3"), X("w3"), 0.0, A.min)
-        lconv("ps1", 256, "w3")
-        cp(X("lst"), X("ps7", 400, 416))
         ls = X("rl%d_%d" % (t, rank))
         cp(ls, X("ps1", 256, 272))
         need("g", [ls], [])
         nloc[0] += send(g, T, topo, core, others, ls[0], [ls[0]] * 3, T.sem["al%d_%d" % (t, rank)], T.sem.loc)
-        ts(X("hm"), X("mb"), -192.0, A.add)
-        act(X("hb"), X("hm"), AF.Abs)
+        cp(X("lst"), X("ps7", 400, 416))
         if not last:
             hash_pe()
+            names()
             act(X("hm"), X("hb"), AF.Copy, bias=-192.0)
         cp(IND(0, YB, X("lst")), X("win", YB, END), extra=[X("lst")])
-        tt(X("oh"), X("ohK"), X("gor"), A.mult)
-        cp(X("Di"), X("ps6", 400, 416))
         if not last:
-            op("v", [X("ps6", 416, 432)], [X("cA")], lambda e: e.tensor_reduce(X("cA")[0], X("ps6", 416, 432)[0], AxisListType.X, A.add))
-        tt(X("key"), X("key"), X("oh"), A.add)
-        ts(X("Dm"), X("Di"), 3, A.bitwise_and)
-        ts(X("h0"), X("offb"), float(VAL), A.is_lt)
-        if not last:
-            ts(X("qA"), X("cA"), 1.0 / 64, A.mult, 128.5 + 1.0 / 128, A.add)
-        ts(X("dk"), X("Dm"), 131072.0, A.mult, float(((t + 1) << 17) + (t << 13)), A.add)
-        tt(X("fr"), X("h0"), X("nf"), A.mult)
-        tt(X("m1"), X("offb"), X("nm", t, 256, 16), A.subtract)
-        if not last:
-            ts(X("Acol"), X("qA"), -64.0, A.mult, X("cA"), A.add)
-            hash_q()
-        tt(X("nk"), X("dk"), X("offb"), A.add)
-        tt(X("m2"), X("m1"), X("fr"), A.mult)
-        tt(X("k1"), X("nk"), X("key", t, 256, 16), A.subtract)
-        tt(X("nm", t, 256, 16), X("m2"), X("nm", t, 256, 16), A.add)
-        tt(X("k2"), X("k1"), X("fr"), A.mult)
-        tt(X("key", t, 256, 16), X("k2"), X("key", t, 256, 16), A.add)
-        if not last:
-            places()
-            names()
-            act(X3("nn", 0, 16, 16, 32), X3("nn", 0, 16, 0, 16), AF.Copy)
-            hreps()
-            places2()
-            hits()
-            offsets()
-            drainer(t + 1)
-            same_pe()
-            for gr in range(8):
-                same(gr)
+            address(filler(drainer(t + 1)), False)
+            offsets(False)
+            offsets2()
         else:
             for s in range(16):
                 o, i = X("tmpv", s, 4096, 16), X("win", VAL + 256 * s, VAL + 256 * s + 256)
-                if s % 2:
+                if s % 3:
                     cp(o, i)
                 else:
                     act(o, i, AF.Copy)
             dma("y", T.yval[:], X("tmpv")[0], [X("tmpv")], [])
             dma("y", T.yh[:], X("hb")[0], [X("hb")], [])
-            cp(X("kei"), X("key"))
-            ts(X("key2"), X("kei"), 17, A.logical_shift_right)
-            ts(X("of1"), X("key2"), 31.0, A.min)
-            for hf in range(2):
-                s = (128 * hf, 128 * hf + 128)
-                tr(X("ps4", *s), X("of1", *s), X("I32"))
+            cp(X("z"), X("key"))
+            ts(X("ai"), X("z"), 17, A.logical_shift_right)
+            ts(X("tA"), X("ai"), 31.0, A.min)
+            for hf, s in halves():
+                tr(X("ps4", *s), X("tA", *s), X("I32"))
                 tr(X("ps5", *s), X("nm", *s), X("I32"))
-            act(X("tA"), X("ps4", 0, 256), AF.Copy)
-            act(X("tB"), X("ps5", 0, 256), AF.Copy)
-            dma("y", T.ydue[:], X("tA")[0], [X("tA")], [])
-            dma("y", T.ypnd[:], X("tB")[0], [X("tB")], [])
+            act(X("tB"), X("ps4", 0, 256), AF.Copy)
+            act(X("offP"), X("ps5", 0, 256), AF.Copy)
+            dma("y", T.ydue[:], X("tB")[0], [X("tB")], [])
+            dma("y", T.ypnd[:], X("offP")[0], [X("offP")], [])
         for r in range(len(T.cores) - 1, -1, -1):
             if r != rank:
-                n = bin(topo.mask(T.cores[r], core)).count("1")
+                n = width(topo.mask(T.cores[r], core))
                 wait("v", "av%d_%d" % (t, r), n)
                 wait("v", "al%d_%d" % (t, r), n)
             sv, sl = X("rv%d_%d" % (t, r)), X("rl%d_%d" % (t, r))

from concourse.bass import DstId, RemoteDMATransfer
from concourse.mybir import AluOpType as A, AxisListType, ActivationFunctionType as AF

VAL, TR, YB, END = 8192, 12288, 12544, 12800
F31 = float(31 << 17)
NSTEP = 4
SH = 64
NS1 = 8
HV = 9
SCRATCH = {}


def _d(where, dtype, **k):
    for n, c in k.items():
        SCRATCH[n] = (where, [128] + (list(c) if isinstance(c, (list, tuple)) else [c]), dtype)


_d("sbuf", "bfloat16", win=END, hop=1024, d=4096, ab=4096, hrep=4096, hiS=4096, loS=4096, hiM=2048, loM=2048,
   tmpv=4096, eq=4096, wI=2048, Eb=3072, Wb=128, Ab=128, nAb=128, G8=8, G16=16, Ib=128, n4I=128, n1I=128, nI=128, nEI=128,
   nBI=128, onesb=128, cU=256, KIa=256, KIb=256, CK2=256, tLa=16, tLb=16, hb=256, hm=256, Qb=256, HB=256, mb=256, gor=256,
   fe16=16, qA=1, dkap=128)
for _t in range(NSTEP):
    for _r in range(4):
        _d("sbuf", "bfloat16", **{"rv%d_%d" % (_t, _r): 256})
        _d("sbuf", "uint16", **{"rl%d_%d" % (_t, _r): 16})
_d("sbuf", "float16", If=128, FT=512, LF=512, RF=512)
_d("sbuf", "uint16", offN=256, ld=16, lst=16)
_d("sbuf", "int32", wi=1, ki=1, thi=1, pni=256, dui=256, z=256, zb=128, zs=128, ai=256, mi=256, kmi=16, pl=16, sl=16, xi=48,
   rb=32, Di=16, Dm=16, rci=16, fci=1)
_d("sbuf", "float32", ones32=128, I32=128, t32=128, A32=128, segM=256, segK=256, kapB=256, th16=16, iP=16, trP=16,
   yP=16, tl0=16, key=256, nm=256, nn=[16, 32], tA=256, tB=256, Acol=1, cA=1, Eo=256, offP=256,
   kmf=256, e1=16, e2=16, e3=16, R2=[48, 16], R3=[32, 16], dptM=256, d0=16, dsrc=16, dr=16, dy=16, sqx=48, n1=16, nq=16,
   am=512, o1=16, offb=16, eqd=16, dyE=16, hv=16, a1=16, a2=16, a3=16, nf=16, r1=16, md=256, ms=256, w3=256,
   dk=16, nk=16, h0=16, fr=16, k1=16, k2=16, m1=16, m2=16, ft=16, sL=1, bL=1, sR=1, bR=1, s3=1, fcf=1,
   wf=1, kf=1, tf=1, s13=1)
PACK = {}


def _pack(dtype, big):
    at = 0
    for n in [n for n, v in SCRATCH.items() if v[2] == dtype and len(v[1]) == 2 and v[1][1] <= 64]:
        PACK[n] = (big, at, SCRATCH[n][1][1])
        at += (SCRATCH[n][1][1] + 7) // 8 * 8
        del SCRATCH[n]
    SCRATCH[big] = ("sbuf", [128, at], dtype)


_pack("float32", "pf")
_pack("int32", "pi")
for _b in range(8):
    SCRATCH["ps%d" % _b] = ("psum", [128, 512], "float32")

SEMAPHORES = ["vs", "ss", "pp", "gs", "loc", "locm", "marr", "hop0", "hop1", "hopl"]
SEMAPHORES += ["dm%d" % i for i in range(24)]
SEMAPHORES += [n + "%d_%d" % (t, r) for n in ("av", "al") for t in range(NSTEP) for r in range(4)]


def relay_of(c, T, topo):
    return [x for x in topo.cores_of(c) if topo.die(x) != topo.die(c)
            and all(topo.may_write(x, y) for y in T.cores if y != c)][0]


def width(m):
    return bin(m).count("1")


def send(g, T, topo, src, dsts, src_ap, dst_aps, sem, lsem):
    ids, m = [], topo.mask(src, dsts[0])
    for x in dsts:
        rid, pid, _ = topo.addr(x)
        ids.append(DstId(rid=rid, pnc=pid))
        m &= topo.mask(src, x)
    g.remote_dma_fused([RemoteDMATransfer(dst_ids=ids, dma_engine_mask=m, remote_sem=sem, srcs=[src_ap], dsts=dst_aps)], local_sem=lsem)
    return width(m)


def relay(g, core, T, topo):
    for r, c in enumerate(T.cores):
        if relay_of(c, T, topo) == core:
            oth = [x for x in T.cores if x != c]
            n = 0
            for j in range(2):
                g.wait_ge(T.sem["hop%d" % j], width(topo.mask(c, core)))
                lo = 2048 * r + 1024 + 512 * j
                n += send(g, T, topo, core, oth, T.hop[:, 512 * j:512 * j + 512], [T.win[:, lo:lo + 512]] * 3, T.sem.marr, T.sem.hopl)
            g.wait_ge(T.sem.hopl, n)


def rank_program(g, core, T, topo):
    rank = T.rank_of(core)
    if rank is None:
        relay(g, core, T, topo)
        return
    others = [x for x in T.cores if x != core]
    ENG = {"v": (g.vector, "vs"), "s": (g.scalar, "ss"), "p": (g.tensor, "pp"), "g": (g, "gs"), "y": (g.sync, None)}
    cnt = {"vs": 0, "ss": 0, "pp": 0, "gs": 0}
    waited = {}
    hist = {}
    ndma = [0]
    nloc = [0]

    def X(n, lo=0, hi=None, st=1, p=None):
        big, off, w = PACK[n] if n in PACK else (n, 0, None)
        if w is None:
            w = 512 if n[:2] == "ps" and n[2:].isdigit() else SCRATCH[n][1][1]
        if hi is None:
            hi = w
        ap = T[big][:, off + lo:off + hi:st] if p is None else T[big][p[0]:p[1], off + lo:off + hi:st]
        return (ap, big, off + lo, off + hi, st, (off + lo) % st, (off + lo) % st + 1)

    def X3(n, s0, s1, a, b=None):
        t = T[n]
        w = SCRATCH[n][1][2]
        ap = t[:, s0:s1, a] if b is None else t[:, s0:s1, a:b]
        return (ap, n, s0 * w, s1 * w, w, a, a + 1 if b is None else b)

    def IND(lo, hi, off):
        return (T.win[:, lo:hi].indirect(off[0]), "win", lo, hi, 1, 0, 1)

    def meet(e, f):
        return e[0] < f[1] and f[0] < e[1] and (e[2] != f[2] or (e[3] < f[4] and f[3] < e[4]))

    def wait(q, sem, val):
        if waited.get((q, sem), 0) < val:
            waited[(q, sem)] = val
            ENG[q][0].wait_ge(T.sem[sem], val)

    def need(q, rs, ws):
        deps = {}
        for regs, isw in ((rs, False), (ws, True)):
            for x in regs:
                b = x[1]
                bank = b[:2] == "ps" and b[2:].isdigit()
                for (r2, q2, sem, val, w2) in hist.get(b, []):
                    if bank and q2 != q:
                        hit = True
                    else:
                        hit = meet(x[2:], r2)
                        if q2 == q:
                            hit = hit and w2 and q != "p"
                        else:
                            hit = hit and (w2 or isw)
                    if hit:
                        deps[sem] = max(deps.get(sem, 0), val)
        for sem, val in deps.items():
            wait(q, sem, val)

    def note(q, rs, ws, sem, val):
        for regs, isw in ((rs, False), (ws, True)):
            for x in regs:
                h = hist.setdefault(x[1], [])
                h[:] = [e for e in h if not (e[0] == x[2:] and e[1] == q and e[2] == sem and (isw or not e[4]))]
                h.append((x[2:], q, sem, val, isw))

    def op(q, rs, ws, fn):
        need(q, rs, ws)
        sem = ENG[q][1]
        cnt[sem] += 1
        fn(ENG[q][0]).then_inc(T.sem[sem], 1)
        note(q, rs, ws, sem, cnt[sem])

    def dma(q, out, in_, rs, ws):
        need(q, rs, ws)
        sem = "dm%d" % ndma[0]
        ndma[0] += 1
        ENG[q][0].dma_start(out, in_).then_inc(T.sem[sem], 16)
        note(q + "d", rs, ws, sem, 16)

    def cols(*xs):
        return [x for x in xs if isinstance(x, tuple)]

    def val_(x):
        return x[0] if isinstance(x, tuple) else x

    def tt(o, a, b, f, extra=()):
        op("v", [a, b] + list(extra), [o], lambda e: e.tensor_tensor(o[0], a[0], b[0], f))

    def ts(o, a, s1, f1, s2=None, f2=None):
        if f2 is None:
            op("v", [a] + cols(s1), [o], lambda e: e.tensor_scalar(o[0], a[0], val_(s1), None, f1))
        else:
            op("v", [a] + cols(s1, s2), [o], lambda e: e.tensor_scalar(o[0], a[0], val_(s1), val_(s2), f1, f2))

    def cp(o, a, extra=()):
        op("v", [a] + list(extra), [o], lambda e: e.tensor_copy(o[0], a[0]))

    def ms(o, v):
        op("v", [], [o], lambda e: e.memset(o[0], v))

    def scan(o, a, b, ini, f1, f2):
        op("v", [a, b], [o], lambda e: e.tensor_tensor_scan(o[0], a[0], b[0], ini, f1, f2))

    def act(o, a, f, bias=0.0, scale=1.0, extra=()):
        op("s", [a] + cols(bias, scale) + list(extra), [o], lambda e: e.activation(o[0], a[0], f, bias=val_(bias), scale=val_(scale)))

    def mm(o, l, r, start, stop):
        op("p", [l, r], [o], lambda e: e.matmul(o[0], l[0], r[0], start, stop))

    def tr(o, a, i):
        op("p", [a, i], [o], lambda e: e.transpose(o[0], a[0], i[0]))

    def iota(o, pat, base, cm):
        op("g", [], [o], lambda e: e.iota(o[0], pat, base, cm, allow_small_or_imprecise_dtypes=True))

    def asel(o, a, pat, cmp, fill, base, cm):
        op("g", [a], [o], lambda e: e.affine_select(o[0], a[0], pat, cmp, fill, base, cm))

    lo = 2048 * rank
    own = [X("win", lo + 1024, lo + 1536), X("win", lo + 1536, lo + 2048), X("win", lo, lo + 1024)]
    dma("y", own[0][0], T.mem[:, 1024:1536], [], [own[0]])
    dma("s", own[1][0], T.mem[:, 1536:2048], [], [own[1]])
    dma("y", own[2][0], T.mem[:, 0:1024], [], [own[2]])
    for q, n, src in (("s", "wi", T.w), ("y", "pni", T.pnd), ("s", "hb", T.h), ("y", "dui", T.due), ("s", "ki", T.kap), ("y", "thi", T.th)):
        dma(q, X(n)[0], src[:], [], [X(n)])
    dma("s", X("tmpv")[0], T.val[:], [], [X("tmpv")])
    ms(X("ones32"), 1.0)
    asel(X("I32"), X("ones32"), [[-1, 128]], A.is_equal, 0.0, 0, 1)
    asel(X("t32"), X("ones32"), [[-16, 8], [0, 16]], A.is_ge, 0.0, 0, 1)
    asel(X("A32"), X("t32"), [[16, 8], [0, 16]], A.is_ge, 0.0, 15, -1)
    iota(X("rci"), [[0, 16]], 0, 1)
    iota(X("iP"), [[128, 2], [0, 8]], 0, 1)
    iota(X("fci"), [[0, 1]], 0, 1)
    iota(X("mi"), [[0, 16], [-1, 16]], 16, 1)
    rel = relay_of(core, T, topo)
    nm_ = 0
    for j in range(2):
        need("g", [own[j]], [])
        nm_ += send(g, T, topo, core, [rel], own[j][0], [T.hop[:, 512 * j:512 * j + 512]], T.sem["hop%d" % j], T.sem.locm)
    need("g", [own[2]], [])
    nm_ += send(g, T, topo, core, others, own[2][0], [own[2][0]] * 3, T.sem.marr, T.sem.locm)
    arr = 0
    for x in others:
        y = relay_of(x, T, topo)
        arr += width(topo.mask(x, core)) + 2 * width(topo.mask(y, core))
    for r in range(4):
        hist.setdefault("win", []).append(((2048 * r, 2048 * r + 2048, 1, 0, 1), "x") + (("locm", nm_, False) if r == rank else ("marr", arr, True)))
    iota(X("KIa"), [[128, 2], [0, 8], [256, 16]], -8192, 0)
    iota(X("KIb"), [[0, 256]], 0, 1)
    iota(X("CK2"), [[-16512, 2], [0, 8], [-128, 16]], 18432, 0)
    iota(X("tl0"), [[16, 16]], 0, 0)

    ms(X("onesb"), 1.0)
    ms(X("cU"), 4128.0)
    ms(X("segK"), 0.0)
    ms(X("segK", 0, 256, 16), 16777216.0)
    cp(X("Ib"), X("I32"))
    ts(X("n4I"), X("Ib"), -4096.0, A.mult)
    cp(X("wf"), X("wi"))
    ts(X("Wb"), X("A32"), X("wf"), A.mult)
    ts(X("rci"), X("rci"), 15, A.bitwise_and)
    ts(X("s13"), X("rci", 0, 1), 8192.0, A.mult)
    cp(X("kf"), X("ki"))
    ts(X("dkap"), X("Ib"), X("kf"), A.mult)
    for hf in range(2):
        mm(X("ps2", 128 * hf, 128 * hf + 128), X("onesb"), X("dkap"), True, True)
    cp(X("tA"), X("pni"))
    ts(X("key"), X("dui"), 131072.0, A.mult, X("s13"), A.add)
    tt(X("offP"), X("key"), X("tA"), A.add)
    for hf in range(2):
        s = (128 * hf, 128 * hf + 128)
        tr(X("ps3", s[0] + 256, s[1] + 256), X("tA", *s), X("I32"))
        tr(X("ps3", *s), X("offP", *s), X("I32"))
    act(X("kapB"), X("ps2", 0, 256), AF.Copy)
    cp(X("tf"), X("thi"))
    ts(X("t32"), X("I32"), X("tf"), A.mult)
    cp(X("nm"), X("ps3", 256, 512))
    cp(X("key"), X("ps3", 0, 256))
    for hf in range(2):
        mm(X("ps2", 128 * hf, 128 * hf + 128), X("ones32"), X("t32"), True, True)
    ms(X("Acol"), -0.25)
    for r in range(16):
        act(X("wI", 128 * r, 128 * r + 128), X("Ib"), AF.Copy, scale=256.0 * (64 + r))
    act(X("hm"), X("hb"), AF.Copy, bias=-192.0)

    def double_s(n, s0, s1):
        for a in (1, 2, 4, 8):
            act(X3(n, s0, s1, a, 2 * a), X3(n, s0, s1, 0, a), AF.Copy)

    def halves():
        return [(hf, (128 * hf, 128 * hf + 128)) for hf in range(2)]

    def hash_pe():
        for hf, s in halves():
            mm(X("ps0", *s), X("hb", *s), X("Wb"), True, True)
        mm(X("ps1", 0, 256), X("onesb"), X("cU"), True, False)
        for hf, s in halves():
            mm(X("ps1", *s), X("hb", *s), X("Wb"), False, False)
        act(X("Qb"), X("ps0", 0, 256), AF.Copy, bias=128.5 + 2.0 ** -13, scale=1.0 / 4096)
        mm(X("ps1", 0, 256), X("n4I"), X("Qb"), False, True)

    def names():
        act(X("ps0", 256, 512), X("key"), AF.Relu, bias=(1 - F31) * 16384.0, scale=16384.0)
        act(X("ps5", 256, 512), X("key"), AF.Copy)

    def names2():
        tt(X3("nn", 0, 16, 0, 16), X("ps0", 256, 512), X("nm"), A.add)
        act(X3("nn", 0, 16, 16, 32), X3("nn", 0, 16, 0, 16), AF.Copy)

    def drainer(t):
        scan(X("kmf"), X("segK"), X("key"), 0.0, A.max, A.min)
        k15 = X("kmf", 15, 256, 16)
        yield
        cp(X("kmi"), k15)
        ts(X("e1"), k15, F31, A.is_ge, 4096.0, A.mult)
        ts(X("e2"), k15, float((t + 1) << 17), A.is_lt, -8192.0, A.mult)
        cp(X3("R2", 0, 16, 0), k15)
        yield
        ts(X("pl"), X("kmi"), 8191, A.bitwise_and)
        ts(X("sl"), X("kmi"), 13, A.logical_shift_right, 15, A.bitwise_and)
        tt(X("e3"), X("e1"), X("e2"), A.add)
        yield
        tt(X3("R2", 32, 48, 0), X("pl"), X("trP"), A.subtract)
        ts(X("xi", 0, 16), X("pl"), 8, A.logical_shift_right, 31, A.bitwise_and)
        tt(X3("R2", 16, 32, 0), X("e3"), X("th16"), A.add)
        double_s("R2", 0, 48)
        yield
        ts(X("xi", 16, 32), X("pl"), 4, A.logical_shift_right, 15, A.bitwise_and)
        ts(X("xi", 32, 48), X("pl"), 15, A.bitwise_and)
        ts(X("d0"), X("sl"), 256.0, A.mult, float(VAL), A.add)
        yield
        tt(X("sqx"), X("xi"), X("xi"), A.mult)
        tt(X("dsrc"), X("d0"), X("iP"), A.add)
        cp(X("FT", 0, 512, 32), X("xi", 0, 16))
        yield
        tt(X("n1"), X("sqx", 0, 16), X("sqx", 16, 32), A.add)
        cp(X("FT", 1, 512, 32), X("xi", 16, 32))
        cp(X("FT", 2, 512, 32), X("xi", 32, 48))
        yield
        tt(X("nq"), X("n1"), X("sqx", 32, 48), A.add)
        tt(X("dr"), X("dsrc"), X("trP"), A.subtract)
        tt(X("dy"), X("yP"), X("dsrc"), A.subtract)
        act(X("FT", 3, 512, 32), X("nq"), AF.Copy)
        act(X("FT", 4, 512, 32), X("nq"), AF.Copy)
        same_pe()
        yield

    def drainer2():
        tt(X("dptM"), X("ps3", 256, 512), X3("R2", 32, 48, 0, 16), A.mult)

    def drainer3():
        tt(X("ps4", 256, 512), X("ps5", 256, 512), X3("R2", 0, 16, 0, 16), A.is_equal)
        act(X("ps4", 256, 512), X("ps4", 256, 512), AF.Copy, scale=4194304.0)

    def same_pe():
        for j in range(4):
            mm(X("ps6", 128 * j, 128 * j + 128), X("FT", 128 * j, 128 * j + 128), X("If"), True, True)
        act(X("LF"), X("ps6"), AF.Identity, bias=X("bL"), scale=X("sL"))
        act(X("RF"), X("ps6"), AF.Identity, bias=X("bR"), scale=X("sR"))

    def same(gr):
        q, st = gr % 4, gr // 4
        b = "ps%d" % (6 + gr % 2)
        p = (32 * q, 32 * q + 5)
        b0, b1 = (128 * st, 128 * st + 128), (256 + 128 * st, 384 + 128 * st)
        mm(X(b, 0, 128), X("LF", *b0, p=p), X("RF", *b0, p=p), True, True)
        mm(X(b, 128, 256), X("LF", *b1, p=p), X("RF", *b1, p=p), True, True)
        mm(X(b, 256, 384), X("LF", *b0, p=p), X("RF", *b1, p=p), True, True)
        act(X("Eb", 384 * gr, 384 * gr + 384), X(b, 0, 384), AF.Relu, bias=16384.0, scale=-16384.0)
        e = X("Eb", 384 * gr, 384 * gr + 256)
        asel(e, e, [[0, 2], [1, 128]], A.is_gt, 0.0, 0, -1)

    def address(fill, first):
        mm(X("ps2", 0, 256), X("Ib"), X("KIa"), True, False)
        mm(X("ps2", 0, 256), X("Ib"), X("KIb"), False, False)
        tt(X("tB"), X("ps1", 0, 256), X("kapB"), A.mult)
        act(X("ps1", 0, 256), X("ps1", 0, 256), AF.Square, scale=0.25)
        act(X("tA"), X("tB"), AF.Identity, bias=X("Acol"))
        fill(1)
        names2()
        fill(2)
        tt(X("z"), X("ps1", 0, 256), X("tA"), A.add)
        fill(1)
        ts(X("zb"), X("z", 1, 256, 2), 3, A.logical_shift_right, 1, A.bitwise_and)
        fill(1)
        tt(X("zs"), X("zb"), X("z", 1, 256, 2), A.mult)
        fill(1)
        tt(X("z", 1, 256, 2), X("zs"), X("nm", 1, 256, 2), A.add)
        fill(1)
        ts(X("ai"), X("z"), 8191, A.bitwise_and)
        fill(1)
        cp(X("ps3", 0, 256), X("ai"))
        fill(9)
        if first:
            hrep("s", 0, 11)
        for r in range(16):
            e = X("eq", 256 * r, 256 * r + 256)
            tt(e, X("ps3", 0, 256), X3("nn", 0, 16, r, r + 16), A.is_equal)
            mm(X("ps2", 0, 256), X("wI", 128 * r, 128 * r + 128), e, False, r == 15)
        if first:
            hrep("s", 11, 16)
        drainer2()
        drainer3()
        if not first:
            hrep("v", HV, 12)
        ts(X("Eo"), X("ps2", 0, 256), 12288.0, A.is_ge, -4096.0, A.mult)
        if not first:
            hrep("v", 12, 13)
        tt(X("Eo"), X("Eo"), X("ps2", 0, 256), A.add)

    def offsets(first):
        if not first:
            hrep("v", 13, 14)
        tt(X("offP"), X("Eo"), X("ps3", 0, 256), A.max)
        if not first:
            hrep("v", 14, 16)
        for hf, s in halves():
            tr(X("ps7", *s), X("offP", *s), X("I32"))
        act(X("HB"), X("offP"), AF.Copy, bias=128.5 + 1.0 / 256, scale=1.0 / 128)

    def offsets2():
        cp(X("offN"), X("ps7", 0, 256))
        for hf, s in halves():
            b = "ps%d" % (4 + hf)
            mm(X(b, 0, 256), X("Ib"), X("CK2"), True, False)
            mm(X(b, 0, 128), X("I32"), X("offP", *s), False, False)
            mm(X(b, 0, 128), X("n1I"), X("HB", *s), False, False)
            mm(X(b, 128, 256), X("Ib"), X("HB", *s), False, False)
        for gr in range(NS1):
            same(gr)

    def hrep(q, a, b):
        for k in range(a, b):
            if q == "v":
                cp(X("hrep", k, 4096, 16), X("hb"))
            else:
                act(X("hrep", k, 4096, 16), X("hb"), AF.Copy)

    def lconv(bank, c, src):
        mm(X(bank, c, c + 16), X("Ib"), X("tLa"), True, False)
        mm(X(bank, c, c + 16), X("Ib"), X("tLb"), False, False)
        for hf, s in halves():
            mm(X(bank, c + 8 * hf, c + 8 * hf + 8), X(src, *s), X("A32", 0, 128, 16), False, hf == 1)

    def filler(gen):
        def fill(n):
            for _ in range(n):
                next(gen, None)
        return fill

    def hi(hf):
        s = (2048 * hf, 2048 * hf + 2048)
        scan(X("hiS", *s), X("hiM"), X("d", *s), -200.0, A.min, A.max)

    def lo_(hf):
        s = (2048 * hf, 2048 * hf + 2048)
        scan(X("loS", *s), X("loM"), X("d", *s), 200.0, A.max, A.min)

    def amax(hf):
        scan(X("am", 256 * hf, 256 * hf + 256), X("segM"), X("ps%d" % (4 + hf), 0, 256), 0.0, A.mult, A.max)

    def score(hf):
        b = "ps%d" % (4 + hf)
        for k in range(16):
            mm(X(b, k, 256, 16), X("ab", 2048 * hf + k, 2048 * hf + 2048, 16), X("G16"), False, k == 15)

    hash_pe()
    names()
    cp(X("th16"), X("ps2", 0, 256, 16))
    ts(X("trP"), X("iP"), float(TR), A.add)
    ts(X("yP"), X("iP"), float(YB), A.add)
    ts(X("fci"), X("fci"), 31, A.bitwise_and)
    ms(X("dptM"), 0.0)
    cp(X("fcf"), X("fci"))
    cp(X("FT", 0, 256), X("dptM"))
    cp(X("FT", 256, 512), X("dptM"))
    ts(X("sL"), X("fcf"), 4.0, A.is_lt)
    ts(X("bL"), X("fcf"), 4.0, A.is_equal)
    ts(X("s3"), X("fcf"), 3.0, A.is_lt, -2.0, A.mult)
    ts(X("bR"), X("fcf"), 3.0, A.is_equal)
    tt(X("sR"), X("s3"), X("bL"), A.add)
    cp(X("If"), X("I32"))
    ts(X("mi"), X("mi"), 15, A.bitwise_and)
    ts(X("ps3", 256, 512), X("mi"), 0.0, A.is_equal)
    address(filler(drainer(0)), True)
    ts(X("n1I"), X("Ib"), -128.0, A.mult)
    ts(X("G16", 0, 8), X("A32", 0, 128, 16), 2048.0, A.mult)
    ts(X("G16", 8, 16), X("A32", 0, 128, 16), 2048.0, A.mult)
    offsets(True)
    for s in range(0, 16):
        cp(X("win", VAL + 256 * s, VAL + 256 * s + 256), X("tmpv", s, 4096, 16))
    offsets2()
    ts(X("nI"), X("Ib"), -1.0, A.mult)
    ts(X("nBI"), X("Ib"), -2.0, A.mult)
    ts(X("nEI"), X("Ib"), -16384.0, A.mult)
    cp(X("Ab"), X("A32"))
    ts(X("nAb"), X("A32"), -1.0, A.mult)
    cp(X("G8"), X("A32", 0, 128, 16))
    tt(X("tLb"), X("tl0"), X("rci"), A.add)
    ms(X("tLa"), float(TR))
    ms(X("segM"), 1.0)
    ms(X("segM", 0, 256, 16), 0.0)
    ms(X("hiM"), 200.0)
    ms(X("hiM", 0, 2048, 16), -200.0)
    ms(X("loM"), -200.0)
    ms(X("loM", 0, 2048, 16), 200.0)
    ms(X("win", TR, END), 0.0)

    for t in range(NSTEP):
        last = t == NSTEP - 1
        c1, f1 = 4096 - 16 * SH, 256 - SH
        fs = X("offN", f1, 256)
        act(X("d", c1, 4096), IND(0, TR, fs), AF.Copy, extra=[fs])
        for a, e in ((0, 128), (128, f1)):
            fv, o = X("offN", a, e), X("d", 16 * a, 16 * e)
            tt(o, IND(0, TR, fv), X("hrep", 16 * a, 16 * e), A.subtract, extra=[fv])
        bl = [("ps2", c1), ("ps1", c1 + 512), ("ps0", c1 + 1024)][:SH // 32]
        for b, c in bl:
            mm(X(b), X("nI"), X("hrep", c, c + 512), True, False)
            mm(X(b), X("Ib"), X("d", c, c + 512), False, True)
        act(X("ab", 0, 2048), X("d", 0, 2048), AF.Abs)
        score(0)
        act(X("ab", 2048, c1), X("d", 2048, c1), AF.Abs)
        for b, c in bl:
            act(X("ab", c, c + 512), X(b), AF.Abs)
        score(1)
        for gr in range(NS1, 8):
            same(gr)
        hi(0)
        lo_(0)
        for hf, s in halves()[:1]:
            mm(X("ps0", *s), X("hiS", 15, 2048, 16), X("Ab"), True, False)
            mm(X("ps0", *s), X("loS", 15, 2048, 16), X("nAb"), False, True)
        hi(1)
        amax(0)
        ts(X("ft"), X("iP"), float(VAL + 256 * t), A.add)
        lo_(1)
        s = (128, 256)
        mm(X("ps0", *s), X("hiS", 2063, 4096, 16), X("Ab"), True, False)
        mm(X("ps0", *s), X("loS", 2063, 4096, 16), X("nAb"), False, True)
        mm(X("ps7", 0, 256), X("Ib"), X("hiS", 15, 4096, 16), True, False)
        mm(X("ps7", 0, 256), X("Ib"), X("loS", 15, 4096, 16), False, False)
        mm(X("ps7", f1, 256), X("nBI"), X("hb", f1, 256), False, True)
        amax(1)
        act(X("mb"), X("ps7", 0, 256), AF.Copy, bias=191.75, scale=0.5)
        mm(X("ps6", 0, 256), X("Ib"), X("mb"), True, False)
        mm(X("ps6", 0, 256), X("Ib"), X("hm"), False, True)
        act(X("hb"), X("mb"), AF.Abs, bias=-192.0)
        for hf in range(2):
            cp(X("rb", 16 * hf, 16 * hf + 16), X("am", 256 * hf + 15, 256 * hf + 256, 16))
        tt(X("gor"), X("ps0", 0, 256), X3("R2", 16, 32, 0, 16), A.is_ge)
        mm(X("ps1", 0, 256), X("nEI"), X("gor"), True, False)
        for gr in range(8):
            for hf in range(2):
                o = X("ps1", 128 * hf + 16 * gr, 128 * hf + 16 * gr + 16)
                e = 384 * gr
                mm(o, X("Eb", e + 256 * hf, e + 256 * hf + 128), X("gor", 16 * gr, 16 * gr + 16), False, False)
                if hf:
                    mm(o, X("Eb", e + 128, e + 256), X("gor", 128 + 16 * gr, 144 + 16 * gr), False, gr == 7)
        act(X("win", YB, END), X("ps6", 0, 256), AF.Copy)
        ts(X("rb"), X("rb"), 127, A.bitwise_and)
        tt(X("nf"), X("ps0", 0, 256, 16), X("th16"), A.is_lt)
        for hf in range(2):
            ts(X("o1", 8 * hf, 8 * hf + 8), X("rb", 16 * hf + 8, 16 * hf + 16), 128.0, A.mult, -128.0, A.add)
        tt(X("fe16"), X("ps0", 0, 256, 16), X("th16"), A.is_ge)
        for hf in range(2):
            tt(X("offb", 8 * hf, 8 * hf + 8), X("o1", 8 * hf, 8 * hf + 8), X("rb", 16 * hf, 16 * hf + 8), A.add)
        tt(X("ps4", 256, 512), X("ps4", 256, 512), X("gor"), A.mult)
        tt(X("eqd"), X("offb"), X("dsrc"), A.is_equal)
        tt(X("a1"), X("offb"), X("ft"), A.subtract)
        ts(X("hv"), X("offb"), float(VAL), A.is_ge)
        ts(X("h0"), X("offb"), float(VAL), A.is_lt)
        tt(X("dyE"), X("eqd"), X("dy"), A.mult)
        tt(X("m1"), X("offb"), X("nm", t, 256, 16), A.subtract)
        tt(X("a2"), X("hv"), X("a1"), A.mult)
        tt(X("r1"), X("dyE"), X("nf"), A.mult)
        tt(X("fr"), X("h0"), X("nf"), A.mult)
        ts(X("a3"), X("a2"), float(VAL + 256 * t - TR), A.add)
        tt(X3("R3", 0, 16, 0), X("r1"), X("dr"), A.add)
        tt(X("m2"), X("m1"), X("fr"), A.mult)
        tt(X3("R3", 16, 32, 0), X("a3"), X("nf"), A.mult)
        double_s("R3", 0, 32)
        act(X("ps1", 0, 256), X("ps1", 0, 256), AF.Relu, scale=-1.0 / 16384)
        for hf in range(2):
            mm(X("ps6", 400 + 8 * hf, 408 + 8 * hf), X("win", YB + 128 * hf, YB + 128 * hf + 128), X("G8"), True, True)
        mm(X("ps6", 416, 432), X("onesb"), X("fe16"), True, True)
        tt(X("key"), X("key"), X("ps4", 256, 512), A.add)
        tt(X("nm", t, 256, 16), X("m2"), X("nm", t, 256, 16), A.add)
        if not last:
            hrep("v", 0, HV)
        cp(X("Di"), X("ps6", 400, 416))
        if not last:
            op("v", [X("ps6", 416, 432)], [X("cA")], lambda e: e.tensor_reduce(X("cA")[0], X("ps6", 416, 432)[0], AxisListType.X, A.add))
        tt(X("k1"), X("key", t, 256, 16), X("offb"), A.subtract)
        ts(X("Dm"), X("Di"), 3, A.bitwise_and)
        if not last:
            ts(X("qA"), X("cA"), 1.0 / 64, A.mult, 128.5 + 1.0 / 128, A.add)
            ts(X("cA"), X("cA"), 8255.75, A.add)
        ts(X("dk"), X("Dm"), 131072.0, A.mult, float(((t + 1) << 17) + (t << 13)), A.add)
        tt(X("w3"), X("ps1", 0, 256), X("dptM"), A.mult)
        tt(X("md"), X("ps3", 256, 512), X3("R3", 0, 16, 0, 16), A.mult)
        lconv("ps2", 256, "md")
        lconv("ps1", 256, "w3")
        tt(X("ms"), X("ps3", 256, 512), X3("R3", 16, 32, 0, 16), A.mult)
        lconv("ps7", 400, "ms")
        tt(X("k2"), X("dk"), X("k1"), A.subtract)
        if not last:
            ts(X("Acol"), X("qA"), -64.0, A.mult, X("cA"), A.add)
        tt(X("k2"), X("k2"), X("fr"), A.mult)
        cp(X("ld"), X("ps2", 256, 272))
        tt(X("key", t, 256, 16), X("k2"), X("key", t, 256, 16), A.add)
        dv = X("rv%d_%d" % (t, rank))
        cp(dv, IND(0, END, X("ld")), extra=[X("ld")])
        need("g", [dv], [])
        nloc[0] += send(g, T, topo, core, others, dv[0], [dv[0]] * 3, T.sem["av%d_%d" % (t, rank)], T.sem.loc)
        ls = X("rl%d_%d" % (t, rank))
        cp(ls, X("ps1", 256, 272))
        need("g", [ls], [])
        nloc[0] += send(g, T, topo, core, others, ls[0], [ls[0]] * 3, T.sem["al%d_%d" % (t, rank)], T.sem.loc)
        cp(X("lst"), X("ps7", 400, 416))
        if not last:
            hash_pe()
            names()
            act(X("hm"), X("hb"), AF.Copy, bias=-192.0)
        cp(IND(0, YB, X("lst")), X("win", YB, END), extra=[X("lst")])
        if not last:
            address(filler(drainer(t + 1)), False)
            offsets(False)
            offsets2()
        else:
            for s in range(16):
                o, i = X("tmpv", s, 4096, 16), X("win", VAL + 256 * s, VAL + 256 * s + 256)
                if s % 3:
                    cp(o, i)
                else:
                    act(o, i, AF.Copy)
            dma("y", T.yval[:], X("tmpv")[0], [X("tmpv")], [])
            dma("y", T.yh[:], X("hb")[0], [X("hb")], [])
            cp(X("z"), X("key"))
            ts(X("ai"), X("z"), 17, A.logical_shift_right)
            ts(X("tA"), X("ai"), 31.0, A.min)
            for hf, s in halves():
                tr(X("ps4", *s), X("tA", *s), X("I32"))
                tr(X("ps5", *s), X("nm", *s), X("I32"))
            act(X("tB"), X("ps4", 0, 256), AF.Copy)
            act(X("offP"), X("ps5", 0, 256), AF.Copy)
            dma("y", T.ydue[:], X("tB")[0], [X("tB")], [])
            dma("y", T.ypnd[:], X("offP")[0], [X("offP")], [])
        for r in range(len(T.cores) - 1, -1, -1):
            if r != rank:
                n = width(topo.mask(T.cores[r], core))
                wait("v", "av%d_%d" % (t, r), n)
                wait("v", "al%d_%d" % (t, r), n)
            sv, sl = X("rv%d_%d" % (t, r)), X("rl%d_%d" % (t, r))
            cp(IND(0, YB, sl), sv, extra=[sl])
    o = X("win", lo, lo + 2048)
    dma("y", T.ymem[:], o[0], [o], [])
    for q in ("vs", "ss", "pp", "gs"):
        wait("g", q, cnt[q])
    wait("g", "loc", nloc[0])
    for j in range(ndma[0]):
        wait("g", "dm%d" % j, 16)
